import numpy as np, ml_dtypes
CORES = [66,74,82,90,194,202,210,218]
N = 8
BF = ml_dtypes.bfloat16
W, L, VI, HOP = 2048, 128, 4, 1
def cols(a, j):
    return np.take_along_axis(a, j[:, :, None, :], 3)
def deal(rng, lo, hi, ends=0, two=False):
    o = rng.permutation(W); n = rng.integers(lo, hi + 1, W)
    if two: n = rng.choice(np.array([lo, hi]), W)
    rest = o[(o > 0) & (o < W - 1)]
    if ends == 1: o = np.concatenate([np.array([0, W - 1]), rest]); n[0] = 16
    if ends == 2: o = np.concatenate([np.array([0]), rest[:15], np.array([W - 1]), rest[15:]]); n[:2] = 16
    start = np.add.accumulate(n) - n; nc = int(np.searchsorted(start, W)); start = start[:nc]
    size = np.minimum(n[:nc], W - start); cid = np.repeat(np.arange(nc), size); pos = np.arange(W) - start[cid]
    sl = np.argsort(rng.random((nc, 16)), axis=1); head = o[start + (size * rng.random(nc)).astype(np.int64)]
    if ends == 1: sl[0] = np.concatenate([np.array([0, 15]), 1 + rng.permutation(14)]); head[0] = (W - 1) * int(rng.integers(0, 2))
    if ends == 2: sl[0] = np.concatenate([np.array([0]), 1 + rng.permutation(15)]); sl[1] = np.concatenate([np.array([15]), rng.permutation(15)]); head[0] = 0; head[1] = W - 1
    r = np.zeros(W, np.int64); r[o] = head[cid]
    cl = np.full((16, W), -1, np.int64); cl[sl[cid, pos], r[o]] = o
    return cl, r
def parts(rng):
    x = rng.integers(0, 256, (N, 8, 16, W)); cl = np.zeros((N, 8, 16, W), np.int64); r = np.zeros((N, 8, W), np.int64)
    for a in range(N):
        for g in range(8):
            lo, hi = ((1, 16), (1, 16), (8, 16), (1, 6))[int(rng.integers(0, 4)) if g else 0]
            cl[a, g], r[a, g] = deal(rng, lo, hi)
    o = rng.integers(0, W, (N, 8, 16, L)); z = rng.integers(0, 256, (N, 8, 16, L))
    t = np.stack([rng.integers(1300, 1800, (N, 8)), rng.integers(1000, 1600, (N, 8))], axis=-1)
    return x, cl, r, o, z, t
def hold(rng, x, cl, r, o, z, t, g, q, v):
    P = rng.permutation(W); w = np.arange(W); n = max(q)
    zero = P[:16]; due = P[16:16 + N]; hot = P[16 + N:16 + N + N * n].reshape(N, n)
    x[:, g][:, :, P[:16 + N + N * n]] = 0
    o[:, g] = rng.choice(zero, (N, 16, L)); z[:, g] = 0
    t[:, g, 0] = rng.integers(0, 13, N); t[:, g, 1] = 4080
    for a in range(N):
        k = np.full((16, W), -1, np.int64); k[rng.integers(0, 16, W), w] = w; cl[a, g] = k; r[a, g] = w
        c = hot[a, :q[a % 4]]; x[a, g][:, c] = 1; o[a, g, 0, rng.permutation(L - 1)[:len(c)]] = c
        d = int(t[a, g, 0]) + q[a % 4] + (1 if a % 4 == 3 else 0)
        x[a, g, :, int(due[a])] = (d >> 4) + (np.arange(16) < (d & 15))
        o[(a - HOP * v) % N, g, 0, L - 1] = due[a]
def pack(x, cl, r, o, z, t):
    return {"feat": x.reshape(N, 128, W).astype(np.float32).astype(BF), "memb": cl.reshape(N, 128, W).astype(np.int32), "rep": r.astype(np.int32),
            "fact": o.reshape(N, 128, L).astype(np.int32), "z": z.reshape(N, 128, L).astype(np.float32).astype(BF), "thr": t.astype(np.int32)}
def setup_inputs(rng):
    return pack(*parts(rng))
def setup_inputs_spread(rng):
    x, cl, r, o, z, t = parts(rng)
    x = np.floor(rng.random((N, 8, 16, W)) * np.exp2(rng.integers(0, 9, (N, 8, 1, W)))).astype(np.int64)
    z = np.floor(rng.random((N, 8, 16, L)) * np.exp2(rng.integers(0, 9, (N, 8, 1, L)))).astype(np.int64)
    o = np.minimum(np.floor(W * rng.random((N, 8, 16, L)) ** 3).astype(np.int64), W - 1)
    t = np.minimum(np.exp2(12 * rng.random((N, 8, 2))).astype(np.int64), 4080)
    t[:, :2, 0] = rng.integers(200, 1200, (N, 2))
    hold(rng, x, cl, r, o, z, t, 3, (127, 127, 127, 127), 1)
    hold(rng, x, cl, r, o, z, t, 5, (127, 127, 127, 127), min(VI, N) - 1)
    return pack(x, cl, r, o, z, t)
def setup_inputs_ends(rng):
    x, cl, r, o, z, t = parts(rng)
    x = 255 * np.where(rng.random((N, 8, 1, W)) < 0.6, rng.integers(0, 2, (N, 8, 1, W)), rng.integers(0, 2, (N, 8, 16, W)))
    z = 255 * np.where(rng.random((N, 8, 1, L)) < 0.6, rng.integers(0, 2, (N, 8, 1, L)), rng.integers(0, 2, (N, 8, 16, L)))
    o = np.where(rng.random((N, 8, 16, L)) < 0.7, (W - 1) * rng.integers(0, 2, (N, 8, 16, L)), o)
    far = ((((W - 1) * (W - 1)) >> 5) + W - 1) & (W - 1)
    for a in range(N):
        for g in range(8):
            both = 1 if g % 2 == 0 else 2
            cl[a, g], r[a, g] = deal(rng, 1, 16, both)
            t[a, g, 0] = 4080 if (g + a) % 4 == 1 else 0
            t[a, g, 1] = 4080 if (g + a) % 2 == 0 else 0
            x[a, g, :, far] = 255; x[a, g, :, W - 1] = 255
            if both == 1:
                x[a, g, :, int(r[a, g, 0])] = 255
                for b in (0, L - 1):
                    z[a, g, :, b] = 0; o[a, g, 0, b] = 0; o[a, g, 15, b] = W - 1
            else: x[a, g, :, 0] = 0
            if g == 7:
                z[a, g] = 255; z[a, g, :, L - 1] = 0; o[a, g, :, L - 1] = 0; o[a, g, 15, L - 1] = W - 1; o[a, g, int(rng.integers(0, 16)), :L - 1] = 0
    return pack(x, cl, r, o, z, t)
def setup_inputs_corners(rng):
    x, cl, r, o, z, t = parts(rng); w = np.arange(W)
    for a in range(N):
        for g in range(8):
            kind = (g + a) % 4; how = (3 * g + a) % 8
            if kind == 0: cl[a, g], r[a, g] = deal(rng, 16, 16)
            elif kind == 1:
                k = np.full((16, W), -1, np.int64); k[15 * rng.integers(0, 2, W), w] = w; cl[a, g] = k; r[a, g] = w
            elif kind == 2: cl[a, g], r[a, g] = deal(rng, 1, 16, 0, True)
            else: cl[a, g], r[a, g] = deal(rng, 15, 16)
            if how == 0: o[a, g] = r[a, g][o[a, g]]
            elif how == 1:
                no = np.flatnonzero(r[a, g] != w)
                if len(no): o[a, g] = rng.choice(no, (16, L))
            elif how == 2: o[a, g] = (W - 1) * rng.integers(0, 2, (16, L))
            elif how == 3: o[a, g] = rng.integers(0, W, (1, L))
            elif how == 4: o[a, g] = np.arange(L)[None, :]
            t[a, g, 0] = (1300, 0, 4080, 1600)[(g // 2 + a) % 4]
            t[a, g, 1] = (0, 1300, 4080, 1100)[(g + a // 2) % 4]
    z[..., 0::4] = 0; z[..., 1::4] = 255; z[..., 2::4] = cols(x, o[:, :, 0, 2::4])
    mm = W - 3; oo = W - 21; s = (((mm * oo) >> 5) + mm) & (W - 1)
    for a in range(N):
        n = (17, 16, 127, 40)[a % 4]; cl[a, 6], r[a, 6] = deal(rng, 2, 6)
        c = rng.permutation(np.flatnonzero(r[a, 6] == w))[:n]
        x[a, 6][:, c] = 0; z[a, 6, :, :n] = 255; o[a, 6, 0, :n] = c; t[a, 6, 0] = 4079; t[a, 6, 1] = 0
        k, e = deal(rng, 1, 16, 1); h = int(e[0]); p = np.arange(W)
        p[h] = oo; p[oo] = h; p[W - 1 - h] = mm; p[mm] = W - 1 - h
        cl[a, 7] = np.where(k >= 0, p[np.maximum(k, 0)], -1)[:, p]; r[a, 7] = p[e[p]]
        x[a, 7][:, np.array([int(r[a, 7, W - 1]), int(r[a, 7, W - 5]), oo, s])] = 0; x[a, 7][:, np.array([mm, s + 1])] = 255
        z[a, 7, :, 0] = 255; o[a, 7, :, 0] = oo; t[a, 7, 0] = 1000; t[a, 7, 1] = 4079
        z[a, 7, :, L - 8:] = 255; i = int(rng.integers(0, 16)); z[a, 7, i, L - 8:L - 4] = 240; z[a, 7, i, L - 4:] = 252
        o[a, 7, :, L - 8:L - 4] = W - 1; o[a, 7, :, L - 4:] = W - 5
    return pack(x, cl, r, o, z, t)
def setup_inputs_crowd(rng):
    x, cl, r, o, z, t = parts(rng); f = rng.integers(0, W, 8); f[5] = W - 1
    for g in (0, 1, 5): o[:, g] = f[g]
    o[:, 1, :, L - 1] = rng.integers(0, W, (N, 16))
    o[:, 2] = rng.choice(np.array([0, int(f[2]), W - 1]), (N, 16, L))
    t[:, (0, 1, 2, 5), 0] = rng.integers(0, 200, (N, 4))
    h = int(rng.integers(0, N))
    for g in (3, 4):
        j = int(rng.integers(0, W - 37)); w = j + 37
        P = rng.permutation(W); P = np.concatenate([P[(P != j) & (P != w)], np.array([j, w])])
        c = P[:4 * L]; b = P[4 * L:8 * L]; rest = P[8 * L:]; zero = rest[:16]; y = int(rest[-3])
        for a in range(N):
            x[a, g][:, c] = 128; x[a, g][:, b] = 0; x[a, g][:, zero] = 0; x[a, g][:, np.array([j, w, y])] = 0
            sl = np.sort(np.argsort(rng.random((4 * L, 16)), axis=1)[:, :2], axis=1)
            k = np.full((16, W), -1, np.int64); k[sl[:, 0], c] = b; k[sl[:, 1], c] = c; k[rng.integers(0, 16, len(rest)), rest] = rest
            k[:, y] = -1; k[:, w] = -1; k[0, w] = y; k[15, w] = w
            cl[a, g] = k; r[a, g] = np.arange(W); r[a, g][b] = c; r[a, g, y] = w
            p = (a % 4) * L + np.arange(L)
            o[a, g] = rng.choice(zero, (16, L)); o[a, g, 0] = np.where(rng.random(L) < 0.5, c[p], b[p])
            if g == 4: o[a, g, 0, L - 1] = zero[0]
            z[a, g] = 0
        q = L if g == 3 else L - 1
        t[:, g, 0] = 2047 - max([(v * q) & 127 for v in range(VI)]); t[:, g, 1] = 0
        if g == 3:
            x[h, g][:, np.array([j, w])] = 128; o[h, g, 1] = j
        else:
            d = int(t[h, g, 0]) + ((q & 127) >> 1); x[h, g, :, w] = (d >> 4) + (np.arange(16) < (d & 15)); o[(h - HOP) % N, g, 0, L - 1] = w
    n = W >> 4
    for a in range(N):
        for g in (6, 7):
            K = rng.permutation(W).reshape(16, n); c = K[rng.integers(1, 16, n), np.arange(n)]
            k = np.full((16, W), -1, np.int64); k[:, c] = K; cl[a, g] = k; r[a, g][K] = c[None, :]
            p = rng.permutation(n)[:L]; o[a, g] = K[rng.integers(0, 16, (16, L)), p[None, :]]
            if g == 6:
                x[a, g][:, c] = 0; z[a, g] = 255; t[a, g] = rng.integers(0, 200, 2)
            else:
                x[a, g][:, c] = 255; x[a, g][:, K[0]] = 0; z[a, g] = 0; t[a, g, 0] = int(rng.integers(1000, 3000)); t[a, g, 1] = 4080
    return pack(x, cl, r, o, z, t)
def setup_inputs_ties(rng):
    x, cl, r, o, z, t = parts(rng)
    x = 64 * rng.integers(0, 4, x.shape); z = 64 * rng.integers(0, 4, z.shape)
    for g in range(0, 8, 2):
        few = rng.permutation(W)[:64]; o[:, g] = rng.choice(few, (N, 16, L))
    t = np.stack([64 * rng.integers(20, 28, (N, 8)), 64 * rng.integers(16, 25, (N, 8))], axis=-1)
    hold(rng, x, cl, r, o, z, t, 1, (1, 2, 3, 0), 1)
    hold(rng, x, cl, r, o, z, t, 5, (1, 2, 3, 0), min(VI, N) - 1)
    return pack(x, cl, r, o, z, t)
def check_inputs(d):
    bad = []
    for k, lo, hi in (("feat", 0, 255), ("memb", -1, W - 1), ("rep", 0, W - 1), ("fact", 0, W - 1), ("z", 0, 255), ("thr", 0, 4080)):
        v = np.asarray(d[k]).astype(np.float64)
        if not (np.all(v >= lo) and np.all(v <= hi)): bad.append("range of " + k)
        elif not np.all(v == np.floor(v)): bad.append("whole numbers in " + k)
    if bad: return bad
    cl = np.asarray(d["memb"]).astype(np.int64).reshape(N, 8, 16, W); r = np.asarray(d["rep"]).astype(np.int64)
    for a in range(N):
        for g in range(8):
            k, c = np.nonzero(cl[a, g] >= 0); m = cl[a, g][k, c]; q = r[a, g]
            if not np.all(np.bincount(m, minlength=W) == 1): bad.append("memb: every column in exactly one class")
            if not np.all(q[m] == c): bad.append("rep and memb agree")
            if not np.all(q[q] == q): bad.append("rep: a representative is a member of its own class")
    return sorted(set(bad))
def reference(feat, memb, rep, fact, z, thr):
    x = feat.astype(np.float32).astype(np.int64).reshape(N, 8, 16, W); cl = memb.astype(np.int64).reshape(N, 8, 16, W); r = rep.astype(np.int64)
    o = fact.astype(np.int64).reshape(N, 8, 16, L); y = z.astype(np.float32).astype(np.int64).reshape(N, 8, 16, L)
    t1 = thr[:, :, 0].astype(np.int64); t2 = thr[:, :, 1].astype(np.int64); A = np.zeros((N, 8), np.int64)
    row = np.arange(16)[None, None, :, None]
    for v in range(VI):
        n = np.take_along_axis(r, o.reshape(N, 8, 16 * L), 2)
        D = np.sum(np.abs(cols(x, n).reshape(N, 8, 16, 16, L) - y[:, :, :, None, :]), axis=2)
        n = n.reshape(N, 8, 16, L); ks = np.argmax(D, axis=2)[:, :, None, :]
        ds = np.take_along_axis(D, ks, 2)[:, :, 0]; c = np.take_along_axis(n, ks, 2)[:, :, 0]; ob = np.take_along_axis(o, ks, 2)
        want = ds > (t1 + (A & 127))[:, :, None]
        win = np.zeros((N, 8, L), bool)
        for a in range(N):
            for g in range(8):
                win[a, g, np.unique(np.where(want[a, g], c[a, g], W + np.arange(L)), return_index=True)[1]] = True
        win = win & want
        m = cols(cl, c); has = (m >= 0) & win[:, :, None, :]; mm = np.maximum(m, 0)
        s = (((mm * ob) >> 5) + mm) & (W - 1)
        both = np.minimum(cols(x, mm.reshape(N, 8, 16 * L)), cols(x, s.reshape(N, 8, 16 * L))).reshape(N, 8, 16, 16, L)
        e = np.sum(np.abs(both - y[:, :, :, None, :]), axis=2)
        keep = has & (e <= t2[:, :, None, None]); gone = has & ~keep; got = np.any(keep, axis=2)
        best = np.argmin(np.where(keep, e, 2 ** 20), axis=2)[:, :, None, :]
        cp = np.where(got, np.take_along_axis(mm, best, 2)[:, :, 0], 0)
        ynew = np.where(got[:, :, None, :], (y + cols(x, cp)) >> 1, np.abs(y - cols(x, c)))
        for a in range(N):
            for g in range(8):
                k = cl[a, g]; k[:, c[a, g][win[a, g]]] = -1
                ex = m[a, g][gone[a, g]]; k[0, ex] = ex; r[a, g, ex] = ex
                b = np.flatnonzero(got[a, g]); k[:, cp[a, g][b]] = np.where(keep[a, g][:, b], m[a, g][:, b], -1)
                i, b = np.nonzero(keep[a, g]); r[a, g, m[a, g][i, b]] = cp[a, g][b]
        u = np.sum(y, axis=2)[:, :, None, :]
        o = np.where(D > t1[:, :, None, None], (((o * u) >> 5) + o + 37 * row) & (W - 1), o)
        y = ynew; A = A + np.sum(win, axis=2)
        if v < VI - 1: o = np.roll(o, HOP, axis=0); y = np.roll(y, HOP, axis=0)
    yc = np.sum((cl + 1) * (row + 1), axis=2)
    return {"yc": yc.astype(np.float32), "yr": r.astype(np.float32), "yo": o.reshape(N, 128, L).astype(np.float32), "yz": y.reshape(N, 128, L).astype(np.float32)}

@@ -1,0 +1,650 @@
+from concourse.mybir import AluOpType, ActivationFunctionType
+
+F32, BF, H, I32, U16 = "float32", "bfloat16", "float16", "int32", "uint16"
+W, L, VI = 2048, 128, 4
+SCRATCH = {}
+
+
+def _sb(dtype, cols, names):
+    for n in names.split():
+        SCRATCH[n] = ("sbuf", [128, cols], dtype)
+
+
+_sb(BF, 4240, "XW")
+_sb(BF, 2048, "XR OH Xg Ym ab")
+_sb(I32, 2048, "M0 R0B")
+_sb(F32, 2048, "MM1 io0 dead")
+_sb(F32, 2176, "TT")
+_sb(H, 2048, "Wg")
+_sb(BF, 512, "E32")
+_sb(BF, 576, "Ga Gb")
+_sb(I32, 128, "Rin fin pi si qi")
+_sb(F32, 128, "Rf Rt Bt ones32 I32 rowA mask32 BB32 D1 rs1 MT diff d1 LP sel old vz5 dz za hb xx xn base "
+              "pf w0 w1 kc yy yS LN zs S0T OHo OLb m0")
+_sb(F32, 256, "SC")
+_sb(F32, 144, "D3 rs3 pm3 df3 d13 SC3 kS I136f")
+_sb(BF, 128, "BBu BBb Ib Inh Ih zin z0 z1 z2 z3 zo0 zo1 zo2 zo3 nzT nf nh emp nwin winb Xn nwB zero")
+_sb(H, 128, "BBh BB16 I16 rowA16 Of LM c0g Pv")
+_sb(BF, 144, "I136b Wb Wbn one5")
+_sb(H, 144, "SV Wn W1")
+_sb(U16, 128, "R0l Rl mu su f0 f1 f2 f3 fo0 fo1 fo2 ul")
+_sb(I32, 64, "it")
+_sb(F32, 128, "cs")
+_sb(BF, 16, "Bw")
+_sb(H, 32, "Bh")
+_sb(I32, 8, "th8")
+BANKS = "pD0 pD1 pK pA pB pC pE pL".split()
+for _n in BANKS:
+    SCRATCH[_n] = ("psum", [128, 512], F32)
+
+SEMAPHORES = (["sV", "sS", "sP", "sG", "sent"] + ["d%d" % i for i in range(24)]
+              + ["aF1", "aF2", "aF3", "aZ1", "aZ2", "aZ3"])
+M1 = 12582912.0
+M2 = 25165824.0
+CYC, GATH, SCAT, PECYC, HOP, FAR = 0.00104, 1.56, 3.8, 0.00053, 0.14, 2.6
+ROUNDS = 900
+OPT = {"g30": "VSSS", "g3": "VSVB", "g2": "SSSB", "g4": "SVSS", "zs": 1, "dz": 1, "base": 0, "lp": 1}
+ORDER = []
+
+
+def arrange(ops):
+    n = len(ops)
+    pred = [set() for _ in ops]
+    lastw, readers, lastp, users, closer = {}, {}, {}, {}, {}
+    for i, o in enumerate(ops):
+        for x in o["r"] + o["w"]:
+            if x in lastw:
+                pred[i].add(lastw[x])
+        for x in o["w"]:
+            pred[i].update(readers.get(x, []))
+        if o["e"] == "P":
+            for b in o["b"]:
+                if b in lastp:
+                    pred[i].add(lastp[b])
+                lastp[b] = i
+                if o["open"]:
+                    pred[i].update(users.get(b, []))
+                    users[b] = []
+        else:
+            for b in o["b"]:
+                users.setdefault(b, []).append(i)
+                assert not ops[lastp[b]]["open"]
+                if closer.get(b) is not None:
+                    pred[i].add(closer[b])
+        if o["e"] == "P" and o["shut"]:
+            closer[o["b"][0]] = i
+        if o["e"] in "GY" or o["kind"] == "dma":
+            if o["e"] in lastp:
+                pred[i].add(lastp[o["e"]])
+            lastp[o["e"]] = i
+        for x in o["r"]:
+            readers.setdefault(x, []).append(i)
+        for x in o["w"]:
+            lastw[x] = i
+            readers[x] = []
+        pred[i].discard(i)
+    succ = [[] for _ in ops]
+    for i in range(n):
+        for j in pred[i]:
+            succ[j].append(i)
+
+    def gap(j, i):
+        same_queue = ops[j]["e"] == ops[i]["e"] and (ops[i]["e"] == "P" or (ops[j]["kind"] != "c" and ops[i]["kind"] != "c"))
+        return ops[j]["c"] if same_queue else ops[j]["c"] + ops[j]["lat"]
+
+    c = [o["c"] for o in ops]
+    lat = [o["lat"] for o in ops]
+    fw = [[(j, gap(j, i)) for j in pred[i]] for i in range(n)]
+    bw = [[(i, c[i] + gap(j, i) - c[j]) for i in succ[j]] for j in range(n)]
+
+    def place(key, back):
+        before, after = (bw, pred) if back else (fw, succ)
+        left = [len(x) for x in before]
+        cand = [i for i in range(n) if left[i] == 0]
+        at = [0.0] * n
+        busy = {x: [] for x in list("VSPGY") + BANKS}
+        while cand:
+            i = min(cand, key=lambda x: key[x])
+            cand.remove(i)
+            e = ops[i]["e"]
+            t = max([at[j] + d for j, d in before[i]] + [lat[i] if back else 0.0])
+            lo, hi = (-lat[i], c[i]) if back else (0.0, c[i] + lat[i])
+            spans = [(a, b, 0.0, c[i]) for a, b, _ in busy[e] if b > t]
+            for x in ops[i]["b"]:
+                spans += [(a, b, lo, hi) for a, b, e2 in busy[x] if e2 != e and b > t + lo]
+            moved = True
+            while moved:
+                moved = False
+                for a, b, l, h in spans:
+                    if t + l < b - 1e-9 and t + h > a + 1e-9:
+                        t = b - l
+                        moved = True
+            at[i] = t
+            busy[e].append((t, t + c[i], e))
+            for x in ops[i]["b"]:
+                busy[x].append((t + lo, t + hi, e))
+            for j in after[i]:
+                left[j] -= 1
+                if left[j] == 0:
+                    cand.append(j)
+        return at
+
+    prio = [0.0] * n
+    for j in range(n - 1, -1, -1):
+        prio[j] = max([gap(j, i) + prio[i] for i in succ[j]] + [c[j] + lat[j]])
+    best, seed = None, 1
+    key = [-x for x in prio]
+    for it in range(ROUNDS):
+        at = place(key, False)
+        span = max(at[i] + c[i] + lat[i] for i in range(n))
+        if best is None or span < best[0]:
+            best = (span, at)
+        noise = []
+        seed = (seed * 1103515245 + 12345) % 2147483648
+        mid = seed / 2147483648.0 * best[0]
+        for i in range(n):
+            seed = (seed * 1103515245 + 12345) % 2147483648
+            noise.append((seed / 2147483648.0 - 0.5) * (0.5, 1.5, 3.0)[it % 3] if abs(best[1][i] - mid) < 5.0 else 0.0)
+        back = place([-(best[1][i] + c[i]) + noise[i] for i in range(n)], True)
+        key = [-(back[i] + c[i]) for i in range(n)]
+    return sorted(range(n), key=lambda i: (best[1][i], i)), best[0]
+
+
+def rank_program(g, core, T, topo):
+    rank = T.rank_of(core)
+    if rank is None:
+        return
+    A, AF = AluOpType, ActivationFunctionType
+    nxt = T.cores[(rank + 1) % len(T.cores)]
+    rid, pid = topo.addr(nxt, core)
+    emask = topo.mask(core, nxt)
+    neng = len(topo.engines(core, nxt))
+    V, S, P = g.vector, g.scalar, g.tensor
+    ops = []
+    mark = [0]
+
+    def ind(win, off):
+        mark[0] = 16 * off.shape[1]
+        return win.indirect(off)
+
+    def add(e, r, w, kind, fn, c, lat=HOP):
+        r, w = r.split(), w.split()
+        b = sorted(set(x.split(".")[0] for x in r + w if "." in x))
+        ops.append({"e": e, "r": r, "w": w, "b": b, "kind": kind, "fn": fn, "c": c, "lat": lat})
+
+    def op(e, r, w, fn, out, per=1.0, scat=False):
+        n, mark[0] = mark[0], 0
+        cyc = n * (SCAT if scat else GATH) + 60 if n else max(64, out.shape[1] * per)
+        add(e, r, w, "c", fn, cyc * CYC + (0.17 if e == "G" else 0.03))
+
+    def dma(e, r, w, pairs, lat):
+        add(e, r, w, "dma", pairs, 0.06 * len(pairs), lat)
+
+    def send(src, dst, sem):
+        add("G", src, dst, "send", (src, dst, sem), 0.3, FAR)
+
+    def tt(r, w, out, a, b, o, scat=False):
+        op("V", r, w, lambda: V.tensor_tensor(out, a, b, o), out, 1.0 if "." in r else 2.0, scat)
+
+    def ts(r, w, out, a, s1, o0, s2=None, o1=None):
+        if o1 is None:
+            op("V", r, w, lambda: V.tensor_scalar(out, a, s1, None, o0), out)
+        else:
+            op("V", r, w, lambda: V.tensor_scalar(out, a, s1, s2, o0, o1), out)
+
+    def cp(r, w, out, a, per=1.0):
+        op("V", r, w, lambda: V.tensor_copy(out, a), out, per)
+
+    def ms(w, out, c):
+        op("V", "", w, lambda: V.memset(out, c), out)
+
+    def scan(r, w, out, a, b, o0, o1):
+        op("V", r, w, lambda: V.tensor_tensor_scan(out, a, b, 0.0, o0, o1), out)
+
+    def act(r, w, out, a, f=None, **kw):
+        op("S", r, w, lambda: S.activation(out, a, AF.Identity if f is None else f, **kw), out)
+
+    def mm(r, w, lst, wide=()):
+        def fn():
+            ins = None
+            for (o, l, rh, st, sp) in lst:
+                ins = P.matmul(o, l, rh, st, sp)
+            return ins
+        cyc = sum(max(min(64, x[1].shape[1]), x[2].shape[1]) * (4 if wide is True or i in wide else 1) for i, x in enumerate(lst))
+        add("P", r, w, "c", fn, cyc * PECYC)
+        ops[-1]["open"] = not lst[-1][4]
+        ops[-1]["shut"] = lst[-1][4] and not lst[0][3]
+
+    def iota(w, out, pat, base, cm, flt=True):
+        if flt:
+            op("G", "", w, lambda: g.iota(out, pat, base, cm, allow_small_or_imprecise_dtypes=True), out, 2.0)
+        else:
+            op("G", "", w, lambda: g.iota(out, pat, base, cm), out, 2.0)
+
+    def sel_(r, w, out, a, pat, base, cm):
+        op("G", r, w, lambda: g.affine_select(out, a, pat, A.is_equal, 0.0, base, cm), out, 2.0)
+
+    def ch(q, n=512):
+        return slice(n * q, n * q + n)
+
+    ul = {n: T.ul[:, 8 * i:8 * i + 8] for i, n in enumerate("bc bc3 cmp prm ol sl c0 nl".split())}
+    ul["e32"] = T.ul[:, 64:96]
+    cs = {}
+    o_ = 0
+    for n, k in (("p", 1), ("k", 1), ("k37", 1), ("kp", 1), ("k0", 1), ("v1", 1), ("v3", 1), ("Ac", 1), ("At", 1), ("wn", 1), ("p32", 1), ("a1", 1), ("a2", 1),
+                 ("t12", 2), ("tmp", 2), ("B32", 8), ("Bk", 8), ("Bkn", 8), ("al", 8), ("nw", 8), ("bias", 8), ("c0b", 8),
+                 ("nvl", 8), ("ix", 8), ("t8", 8), ("nx", 8)):
+        cs[n] = T.cs[:, o_:o_ + k]
+        o_ += k
+    th = T.cs[0:8, o_:o_ + 2]
+    Bw1, Bw3, B16, negb = T.Bw[:, 0:8], T.Bw[:, 8:16], T.Bh[:, 0:8], T.Bh[:, 16:24]
+    Xwin = T.XW[:, 128:2176]
+    X2win = T.XW[:, 128:4225]
+    Twin = T.TT[:, 0:2048]
+    r8 = T.rowA[:, 0:8]
+
+    def rin(a):
+        return (T.Rin[ch(a // 2, 32), ch(a % 2, 64)], T.rep[a, :])
+
+    dma("Y", "", "Rin", [rin(a) for a in range(0, 4)], 1.9)
+    dma("S", "", "Rin2 th8", [rin(a) for a in range(4, 8)] + [(T.th8[0:8, 0:2], T.thr[:, :])], 1.9)
+    dma("Y", "", "fin zin", [(T.fin[:, :], T.fact[:, :]), (T.zin[:, :], T.z[:, :])], 2.0)
+    ms("pad", T.XW[:, 2176:2192], 0.0)
+    dma("Y", "", "X", [(Xwin, T.feat[:, :])], 4.0)
+    dma("Y", "", "M0", [(T.M0[:, :], T.memb[:, :])], 8.0)
+    dma("Y", "", "R0B", [(T.R0B[i:128:16, :], T.rep[:, :]) for i in range(16)], 11.0)
+    dma("Y", "pad", "X2 pad", [(T.XW[:, 2177:4225], T.feat[:, :])], 13.0)
+
+    ms("ones32", T.ones32[:, :], 1.0)
+    ms("one5", T.one5[:, :], 1.0)
+    ms("zero", T.zero[:, :], 0.0)
+    iota("it0", T.it[:, 0:1], [[0, 1]], 0, 1, False)
+    iota("it1", T.it[:, 8:16], [[16, 4], [64, 2]], 0, 0, False)
+    sel_("ones32", "I32", T.I32[:, :], T.ones32[:, :], [[-1, 128]], 0, 1)
+    iota("rowA", T.rowA[:, :], [[1, 128]], 0, 0)
+    sel_("ones32", "Bt", T.Bt[0:8, :], T.ones32[0:8, :], [[1, 8], [0, 16]], 0, -1)
+    iota("pi", T.pi[:, :], [[1, 128]], 128, -1, False)
+    sel_("one5", "I136b", T.I136b[:, 0:136], T.one5[:, 0:136], [[16, 8], [1, 17]], -1, -1)
+    iota("io0", T.io0[:, :], [[1, 2048]], 0, 0)
+    iota("TT", T.TT[:, :], [[-1, 2176]], 2048, 0)
+    iota("MT", T.MT[:, :], [[0, 8], [-128, 16]], 2048, -1)
+
+    cp("it0", "p", cs["p"], T.it[:, 0:1])
+    ts("it0", "it2", T.it[:, 1:2], T.it[:, 0:1], 15, A.bitwise_and)
+    cp("it2", "k", cs["k"], T.it[:, 1:2])
+    ts("it0", "it3", T.it[:, 2:3], T.it[:, 0:1], 96, A.bitwise_and)
+    cp("it3", "p32", cs["p32"], T.it[:, 2:3])
+    ts("it1 k", "prm", ul["prm"], T.it[:, 8:16], cs["k"], A.add)
+    ts("rowA p32", "e32", ul["e32"], T.rowA[:, 0:32], cs["p32"], A.add)
+    mm("Bt", "pA.OT", [(T.pA[:, 0:128], T.Bt[0:8, :], T.Bt[0:8, :], True, True)], True)
+    cp("th8", "th", th, T.th8[0:8, 0:2])
+    mm("Bt th", "pC.ol", [(T.pC[:, 0:2], T.Bt[0:8, :], th, True, True)], True)
+    act("pA.OT", "BB32", T.BB32[:, :], T.pA[:, 0:128])
+    act("pC.ol", "t12", cs["t12"], T.pC[:, 0:2])
+    cp("Rin Rin2 prm", "Rf", T.Rf[:, :], ind(T.Rin[:, :], ul["prm"]))
+    op("V", "Rf", "Rt", lambda: V.transpose(T.Rt[:, :], T.Rf[:, :]), T.Rt[:, :])
+    for q in range(4):
+        cp("Rt", "R0l%d" % q, T.R0l[:, q:128:4], T.Rt[:, ch(q, 32)])
+    R0l = "R0l0 R0l1 R0l2 R0l3"
+    cp("fin", "f0", T.f0[:, :], T.fin[:, :])
+    act("zin", "z0", T.z0[:, :], T.zin[:, :], scale=2.0)
+    act("I32", "Inh", T.Inh[:, :], T.I32[:, :], scale=-0.5)
+    act("I32", "Ib", T.Ib[:, :], T.I32[:, :])
+    act("Ib e32", "E32", T.E32[:, :], ind(T.Ib[:, :], ul["e32"]))
+    B_ = T.BB32[:, 0:128:16]
+    act("BB32", "Bw1", Bw1, B_, scale=32768.0)
+    cp("I32", "I16", T.I16[:, :], T.I32[:, :])
+    act("t12", "tmp", cs["tmp"][:, 0:1], cs["t12"][:, 0:1], scale=-32768.0, bias=-1024.0)
+    act("k tmp", "v1", cs["v1"], cs["k"], scale=-2048.0, bias=cs["tmp"][:, 0:1])
+    act("I32 v1", "D1", T.D1[:, :], T.I32[:, :], scale=cs["v1"])
+    ms("rs1", T.rs1[:, :], 0.0)
+    ms("rs1", T.rs1[:, 0:128:16], -1e12)
+    ts("pi", "si", T.si[:, :], T.pi[:, :], 15, A.bitwise_and)
+    ts("si", "mask32", T.mask32[:, :], T.si[:, :], 0.0, A.is_equal)
+    cp("BB32", "B16", B16, B_)
+    ts("rowA", "bc", ul["bc"], r8, 16.0, A.mult, 15.0, A.add)
+    act("BB32", "B32", cs["B32"], B_)
+    act("BB32", "Bw3", Bw3, B_, scale=262144.0)
+    act("BB32", "BBu", T.BBu[:, :], T.BB32[:, :], scale=1.0 / 64)
+    act("BB32", "BBb", T.BBb[:, :], T.BB32[:, :])
+    act("I32", "Ih", T.Ih[:, :], T.I32[:, :], scale=-32768.0)
+    act("k", "k37", cs["k37"], cs["k"], scale=37.0, bias=-31.0 / 64)
+    act("k", "kp", cs["kp"], cs["k"], bias=1.0)
+    ts("k", "k0", cs["k0"], cs["k"], 0.0, A.is_equal, -1.0, A.mult)
+    act("kp BB32", "Bk", cs["Bk"], B_, scale=cs["kp"])
+    act("Bk", "Bkn", cs["Bkn"], cs["Bk"], scale=-1.0)
+    ts("BB32", "BBh", T.BBh[:, :], T.BB32[:, :], 256.0, A.mult)
+    ts("BB32", "BB16", T.BB16[:, :], T.BB32[:, :], -1.0, A.mult)
+    cp("rowA", "rowA16", T.rowA16[:, :], T.rowA[:, :])
+    act("rowA k", "t8", cs["t8"], r8, scale=16.0, bias=cs["k"])
+    act("t8", "al", cs["al"], cs["t8"], bias=2048.0)
+    ts("t8", "negb", negb, cs["t8"], -1.0, A.mult, -64.0, A.add)
+    ts("rowA", "bc3", ul["bc3"], r8, 17.0, A.mult, 16.0, A.add)
+    ts("rowA kp", "cmp", ul["cmp"], r8, 17.0, A.mult, cs["kp"], A.add)
+    ms("Wb", T.Wb[:, :], 0.0)
+    act("BB32", "Wb", T.Wb[:, 15:143:16], B_, scale=256.0)
+    act("Wb", "Wbn", T.Wbn[:, :], T.Wb[:, :], scale=-1.0)
+    ts("Wb", "Wn", T.Wn[:, :], T.Wb[:, :], -1.0, A.mult)
+    ts("Wb", "W1", T.W1[:, :], T.Wb[:, :], 1.0 / 256, A.mult)
+    ms("I136b", T.I136b[:, 0:136:17], 0.0)
+    act("I136b", "I136f", T.I136f[:, 0:136], T.I136b[:, 0:136])
+    act("t12", "tmp2", cs["tmp"][:, 1:2], cs["t12"][:, 1:2], scale=-262144.0, bias=-16384.0 * 15.5)
+    act("k tmp2", "v3", cs["v3"], cs["k"], scale=16384.0, bias=cs["tmp"][:, 1:2])
+    act("I136b v3", "D3", T.D3[:, 0:136], T.I136b[:, 0:136], scale=cs["v3"])
+    act("I136b", "I136b", T.I136b[:, 0:136], T.I136b[:, 0:136], scale=2147483648.0)
+    ms("SV", T.SV[:, 0:136], 128.0)
+    ts("p ones32", "SV", T.SV[:, 0:136:17], T.ones32[:, 0:8], cs["p"], A.mult)
+    ms("rs3", T.rs3[:, :], 0.0)
+    ms("rs3", T.rs3[:, 0:136:17], 1e12)
+    ms("Ac", cs["Ac"], 0.0)
+    ms("At", cs["At"], 0.0)
+
+    XRall = "XR0 XR1 XR2 XR3 XR0h XR1h XR2h XR3h"
+    MMall = "MM0 MM1 MM2 MM3"
+    OHall = "OH0 OH1 OH2 OH3"
+
+    def gather(e, r, w, out, src):
+        if e == "V":
+            cp(r, w, out, src)
+        else:
+            act(r, w, out, src)
+
+    def piece(e, r, dst, q, win, lst):
+        w = "%s%d" % (dst, q)
+        if e == "B":
+            gather("V", r, w, T[dst][:, ch(2 * q, 256)], ind(win, lst[:, ch(2 * q, 16)]))
+            gather("S", r, w + "h", T[dst][:, ch(2 * q + 1, 256)], ind(win, lst[:, ch(2 * q + 1, 16)]))
+        else:
+            gather(e, r, w + " " + w + "h", T[dst][:, ch(q)], ind(win, lst[:, ch(q, 32)]))
+
+    def diff_mm(src, q, b):
+        mm("nzT E32", b + ".x", [(T[b][:, :], T.nzT[ch(q, 32), :], T.E32[ch(q, 32), :], True, False)])
+        mm("%s%d %s%dh Ib" % (src, q, src, q), b + ".x", [(T[b][:, :], T.Ib[:, :], T[src][:, ch(q)], False, True)])
+
+    def absp(q, b):
+        act(b + ".x", "ab%d" % q, T.ab[:, ch(q)], T[b][:, :], AF.Abs)
+
+    def sum_mm(q, reg, first, step, Bw, name):
+        mm("ab%d %s" % (q, name), reg, [(T.pK[ch(q, 32), first + k:first + k + 7 * step + 1:step], T.ab[:, 512 * q + k:512 * q + 512:16], Bw,
+                                         False, False) for k in range(16)])
+
+    def shut(reg, out):
+        mm("zero Ib", reg, [(out, T.Ib[:, :], T.zero[:, :], False, True)])
+
+    def diag(out, Wd, src, first, stop):
+        return [(out, Wd[:, 15 - r:143 - r], src[:, r:128:16], first and r == 0, stop and r == 15) for r in range(16)]
+
+    def g1(q):
+        tt("TT %s OH%d" % (R0l, q), "Wg%d" % q, T.Wg[:, ch(q)], ind(Twin, T.R0l[:, ch(q, 32)]), T.OH[:, ch(q)], A.mult)
+
+    DB = ("pD0", "pD1")
+    for q, e in ((0, "V"), (2, "S"), (1, "V"), (3, "S")):
+        gather(e, "X " + R0l, "XR%d" % q, T.XR[:, ch(q)], ind(Xwin, T.R0l[:, ch(q, 32)]))
+    for q in range(4):
+        cp("M0 " + R0l, "MM%d" % q, T.MM1[:, ch(q)], ind(T.M0[:, :], T.R0l[:, ch(q, 32)]))
+    for q in range(8):
+        tt("M0 io0 " + R0l, "OH%d" % (q // 2), T.OH[:, ch(q, 256)], ind(T.M0[:, :], T.R0l[:, ch(q, 16)]), T.io0[:, ch(q, 256)], A.is_equal)
+
+    for v in range(VI):
+        f, z = "f%d" % v, "z%d" % v
+        last = v == VI - 1
+        cp(f, "Of", T.Of[:, :], T[f][:, :], 0.5)
+        mm("Of I16", "pA.OT", [(T.pA[:, 0:128], T.Of[:, :], T.I16[:, :], True, True)])
+        mm(z + " Inh", "pB.z", [(T.pB[:, 384:512], T[z][:, :], T.Inh[:, :], True, True)])
+        act("pB.z", "nzT", T.nzT[:, :], T.pB[:, 384:512])
+        mm("ones32 D1", "pK.1", [(T.pK[:, 0:128], T.ones32[:, :], T.D1[:, :], True, False)], True)
+        mm(z + " BBu", "pB.u", [(T.pB[:, 0:128], T.BBu[:, :], T[z][:, :], True, True)])
+        tt("Of pB.u", "pf", T.pf[:, :], T.Of[:, :], T.pB[:, 0:128], A.mult)
+        act(z, "vz5", T.vz5[:, :], T[z][:, :], scale=0.5, bias=-0.5)
+        act("pf k37", "w0", T.w0[:, :], T.pf[:, :], bias=cs["k37"])
+        act("w0", "w1", T.w1[:, :], T.w0[:, :], bias=M1)
+
+        for q, e in enumerate(OPT["g30"] if v == 0 else OPT["g3"]):
+            piece(e, XRall + " " + f, "Xg", q, T.XR[:, :], T[f])
+            diff_mm("Xg", q, DB[q % 2])
+            absp(q, DB[q % 2])
+            sum_mm(q, "pK.1", 0, 16, Bw1, "Bw1")
+        shut("pK.1", T.pK[:, 0:128])
+
+        key = T.pK[:, 0:128]
+        scan("pK.1 rs1", "pm", T.SC[:, 0:128], T.rs1[:, :], key, A.add, A.max)
+        tt("pm pK.1", "diff", T.diff[:, :], T.SC[:, 0:128], key, A.subtract)
+        tt("pA.OT diff", "d1", T.d1[:, :], T.pA[:, 0:128], T.diff[:, :], A.subtract)
+        act("pK.1", "nf", T.nf[:, :], key, AF.Relu, scale=-1.0)
+        scan("diff d1", "os", T.SC[:, 128:256], T.diff[:, :], T.d1[:, :], A.min, A.max)
+        tt("os bc mask32", "LM", T.LM[:, :], ind(T.SC[:, 128:256], ul["bc"]), T.mask32[:, :], A.mult)
+        mm("LM B16", "pC.ol", [(T.pC[:, 0:8], T.LM[:, :], B16, True, True)])
+        act("os bc", "OLb", T.OLb[:, :], ind(T.SC[:, 128:256], ul["bc"]), bias=32.0)
+        mm("OLb I32", "pE.oB", [(T.pE[:, 384:512], T.OLb[:, :], T.I32[:, :], True, True)], True)
+        cp("pC.ol", "ol", ul["ol"], T.pC[:, 0:8])
+        act("pE.oB", "sel", T.sel[:, :], T.pE[:, 384:512])
+        ts(MMall + " ol", "mu", T.mu[:, :], ind(T.MM1[:, :], ul["ol"]), 0.0, A.max)
+        act(MMall + " ol", "m0", T.m0[:, :], ind(T.MM1[:, :], ul["ol"]))
+        tt(MMall + " ol sel", "pi", T.pi[:, :], ind(T.MM1[:, :], ul["ol"]), T.sel[:, :], A.mult)
+        ts("pi", "si", T.si[:, :], T.pi[:, :], 5, A.arith_shift_right, 2047, A.bitwise_and)
+        cp("si", "su", T.su[:, :], T.si[:, :])
+
+        mm("nf Ih w1 I32 Of I16", "pB.f", [(T.pB[:, 128:256], T.I32[:, :], T.w1[:, :], True, False),
+                                           (T.pB[:, 128:256], T.I16[:, :], T.Of[:, :], False, False),
+                                           (T.pB[:, 128:256], T.nf[:, :], T.Ih[:, :], False, True)], (0,))
+        tt("pB.f Of", "qi", T.qi[:, :], T.pB[:, 128:256], T.Of[:, :], A.max)
+        ts("qi", "fin", T.fin[:, :], T.qi[:, :], 2047, A.bitwise_and)
+        if last:
+            cp("fin", "w0", T.w0[:, :], T.fin[:, :])
+            dma("Y", "w0", "", [(T.yo[:, :], T.w0[:, :])], 2.0)
+        else:
+            cp("fin", "fo%d" % v, T["fo%d" % v][:, :], T.fin[:, :])
+            send("fo%d" % v, "f%d" % (v + 1), "aF%d" % (v + 1))
+
+        cp("R0B ol", "c0g", T.c0g[:, :], ind(T.R0B[:, :], ul["ol"]))
+        mm("c0g Wn", "pC.c0", diag(T.pC[:, 24:32], T.Wn, T.c0g, True, True))
+        ts("pC.c0", "c0", ul["c0"], T.pC[:, 24:32], -1.0 / 4096, A.mult)
+        act("pC.c0", "c0b", cs["c0b"], T.pC[:, 24:32], scale=-1.0 / 4096)
+        if v == 0:
+            ts("c0g k0", "Pv", T.Pv[:, :], T.c0g[:, :], -2048.0, A.add, cs["k0"], A.mult)
+        else:
+            act(OHall + " ol", "OHo", T.OHo[:, :], ind(T.OH[:, :], ul["ol"]))
+            tt("TT c0 OHo", "Pv", T.Pv[:, :], ind(Twin, ul["c0"]), T.OHo[:, :], A.mult)
+        act("TT c0", "old", T.old[:, :], ind(Twin, ul["c0"]))
+        mm("Pv BB16 old I32", "pL.vB", [(T.pL[:, 256:384], T.BB16[:, :], T.Pv[:, :], True, False),
+                                        (T.pL[:, 256:384], T.I32[:, :], T.old[:, :], False, True)], (1,))
+        act("pL.vB", "nh", T.nh[:, :], T.pL[:, 256:384], AF.Abs)
+        mm("Pv BBh I16 rowA16", "pE.VA", [(T.pE[:, 0:128], T.I16[:, :], T.rowA16[:, :], True, False),
+                                          (T.pE[:, 0:128], T.BBh[:, :], T.Pv[:, :], False, True)])
+        act("m0", "emp", T.emp[:, :], T.m0[:, :], AF.Relu, scale=-1.0)
+        if OPT["lp"]:
+            act("pm bc", "LP", T.LP[:, :], ind(T.SC[:, 0:128], ul["bc"]))
+            mm("LP I32", "pE.pm", [(T.pE[:, 128:256], T.LP[:, :], T.I32[:, :], True, True)], True)
+            act("pE.pm Ac", "nwB", T.nwB[:, :], T.pE[:, 128:256], AF.Relu, scale=-1.0, bias=cs["Ac"])
+            mm("nwB Wbn", "pC.v", diag(T.pC[:, 16:24], T.Wbn, T.nwB, True, False))
+            mm("Pv Wn I16 negb", "pC.v", [(T.pC[:, 16:24], T.I16[:, :], negb, False, False)] + diag(T.pC[:, 16:24], T.Wn, T.Pv, False, True))
+            act("pC.v", "bias", cs["bias"], T.pC[:, 16:24])
+        else:
+            tt("pm bc mask32", "LP", T.LP[:, :], ind(T.SC[:, 0:128], ul["bc"]), T.mask32[:, :], A.mult)
+            mm("LP B32", "pC.pm", [(T.pC[:, 8:16], T.LP[:, :], cs["B32"], True, True)], True)
+            mm("Pv Wn I16 negb", "pC.v", [(T.pC[:, 16:24], T.I16[:, :], negb, True, False)] + diag(T.pC[:, 16:24], T.Wn, T.Pv, False, True))
+            ts("pC.pm Ac", "nw", cs["nw"], T.pC[:, 8:16], cs["Ac"], A.is_le, -4194304.0, A.mult)
+            tt("pC.v nw", "bias", cs["bias"], T.pC[:, 16:24], cs["nw"], A.add)
+        act("pC.v", "nvl", cs["nvl"], T.pC[:, 16:24], AF.Relu, scale=64.0)
+
+        mm("ones32 D3", "pK.3", [(T.pK[:, 128:264], T.ones32[:, :], T.D3[:, 0:136], True, False)], True)
+        for q in range(4):
+            piece(OPT["g4"][q], "X mu", "Xg", q, Xwin, T.mu)
+            tt("X su Xg%d Xg%dh" % (q, q), "Ym%d" % q, T.Ym[:, ch(q)], ind(Xwin, T.su[:, ch(q, 32)]), T.Xg[:, ch(q)], A.min)
+            diff_mm("Ym", q, DB[q % 2])
+            absp(q, DB[q % 2])
+            if q == 3:
+                mm("emp I136b", "pK.3", [(T.pK[:, 128:264], T.emp[:, :], T.I136b[:, 0:136], False, False)])
+            sum_mm(q, "pK.3", 129, 17, Bw3, "Bw3")
+        mm("nh I136b", "pK.3", [(T.pK[:, 128:264], T.nh[:, :], T.I136b[:, 0:136], False, True)])
+        mm("m0 I136f I16 SV", "pA.val", [(T.pA[:, 128:264], T.m0[:, :], T.I136f[:, 0:136], True, False),
+                                         (T.pA[:, 128:264], T.I16[:, :], T.SV[:, 0:136], False, True)], (0,))
+
+        off = [0]
+        for q in range(8):
+            off.append(off[-1] + 128 - 16 * q)
+        for q in range(8):
+            act("pE.VA bias", "Ga%d" % q, T.Ga[:, off[q]:off[q + 1]], T.pE[:, 16 * q:128], AF.Abs, bias=cs["bias"][:, q:q + 1])
+        act(" ".join("Ga%d" % q for q in range(8)), "Gb", T.Gb[:, :], T.Ga[:, :], AF.Relu, scale=-1.0, bias=65.0)
+        mm("Gb BBb zero", "pE.cnt", [(T.pE[:, 256:384], T.BBb[:, :], T.zero[:, :], True, False)]
+           + [(T.pE[:, 256 + 16 * q:384], T.BBb[:, :], T.Gb[:, off[q]:off[q + 1]], False, q == 0) for q in range(7, -1, -1)])
+        act("pE.cnt", "nwin", T.nwin[:, :], T.pE[:, 256:384], AF.Abs, bias=-1.0)
+        mm("c0b nvl I32 nwin Wb", "pC.R2",
+           [(T.pC[:, 32:40], T.I32[:, :], cs["c0b"], True, False), (T.pC[:, 32:40], T.I32[:, :], cs["nvl"], False, False)]
+           + diag(T.pC[:, 32:40], T.Wb, T.nwin, False, True), (0, 1))
+        tt("pC.R2 al", "ix", cs["ix"], T.pC[:, 32:40], cs["al"], A.min)
+        cp("ix", "sl", ul["sl"], cs["ix"])
+
+        if OPT["dz"]:
+            act(XRall + " ol", "Xn", T.Xn[:, :], ind(T.XR[:, :], ul["ol"]))
+            mm("Xn Ib Inh " + z, "pA.z", [(T.pA[:, 384:512], T.Inh[:, :], T[z][:, :], True, False),
+                                          (T.pA[:, 384:512], T.Ib[:, :], T.Xn[:, :], False, True)])
+            act("pA.z", "Xn", T.Xn[:, :], T.pA[:, 384:512], AF.Abs, scale=2.0)
+            mm("Xn Ib Inh " + z, "pA.z", [(T.pA[:, 384:512], T.Inh[:, :], T[z][:, :], True, False),
+                                          (T.pA[:, 384:512], T.Ib[:, :], T.Xn[:, :], False, True)])
+            act("pA.z", "Y", T.XW[:, 0:128], T.pA[:, 384:512], bias=0.5)
+        else:
+            tt(XRall + " ol vz5", "dz", T.dz[:, :], ind(T.XR[:, :], ul["ol"]), T.vz5[:, :], A.subtract)
+            act("dz", "za", T.za[:, :], T.dz[:, :], AF.Abs, scale=2.0, bias=-1.0)
+            tt("za vz5", "Y", T.XW[:, 0:128], T.za[:, :], T.vz5[:, :], A.subtract)
+        if OPT["base"]:
+            mm("old m0 I32 nh Ih", "pL.b", [(T.pL[:, 384:512], T.I32[:, :], T.old[:, :], True, False),
+                                            (T.pL[:, 384:512], T.I32[:, :], T.m0[:, :], False, False),
+                                            (T.pL[:, 384:512], T.Ih[:, :], T.nh[:, :], False, True)], (0, 1))
+            act("pL.b", "xx", T.xx[:, :], T.pL[:, 384:512], AF.Relu, bias=1.0)
+            if OPT["base"] == 1:
+                act("xx", "xn", T.xn[:, :], T.xx[:, :], scale=-1.0)
+                mm("old xn I32", "pL.b", [(T.pL[:, 384:512], T.I32[:, :], T.old[:, :], True, False),
+                                          (T.pL[:, 384:512], T.I32[:, :], T.xn[:, :], False, True)], True)
+                act("pL.b", "base", T.base[:, :], T.pL[:, 384:512])
+            else:
+                tt("old xx", "base", T.base[:, :], T.old[:, :], T.xx[:, :], A.subtract)
+        else:
+            act("nh", "hb", T.hb[:, :], T.nh[:, :], scale=-8192.0, bias=4096.0)
+            tt(MMall + " ol hb", "xx", T.xx[:, :], ind(T.MM1[:, :], ul["ol"]), T.hb[:, :], A.min)
+            act("xx", "xn", T.xn[:, :], T.xx[:, :], scale=-1.0, bias=-1.0)
+            tt("TT c0 xn", "base", T.base[:, :], ind(Twin, ul["c0"]), T.xn[:, :], A.min)
+
+        key3 = T.pK[:, 128:264]
+        scan("pK.3 rs3", "pm3", T.pm3[:, 0:136], T.rs3[:, 0:136], key3, A.add, A.min)
+        tt("pm3 pK.3", "df3", T.df3[:, 0:136], key3, T.pm3[:, 0:136], A.subtract)
+        act("pK.3", "kS", T.kS[:, 0:136], key3)
+        tt("pA.val df3", "d13", T.d13[:, 0:136], T.pA[:, 128:264], T.df3[:, 0:136], A.subtract)
+        act("kS cmp", "kc", T.kc[:, :], ind(T.kS[:, 0:136], ul["cmp"]))
+        scan("df3 d13", "SC3", T.SC3[:, 0:136], T.df3[:, 0:136], T.d13[:, 0:136], A.min, A.max)
+        tt("SC3 bc3 kc", "yy", T.yy[:, :], ind(T.SC3[:, 0:136], ul["bc3"]), T.kc[:, :], A.max)
+        mm("yy I32", "pB.y", [(T.pB[:, 256:384], T.yy[:, :], T.I32[:, :], True, True)], True)
+        act("pB.y", "yS", T.yS[:, :], T.pB[:, 256:384], scale=-1.0, bias=2176.0)
+        tt("yS base sl", "TT", ind(T.TT[:, :], ul["sl"]), T.yS[:, :], T.base[:, :], A.max, True)
+        tt("SC3 bc3 mask32", "LN", T.LN[:, :], ind(T.SC3[:, 0:136], ul["bc3"]), T.mask32[:, :], A.mult)
+        mm("nwin Wbn", "pL.n", diag(T.pL[:, 128:136], T.Wbn, T.nwin, True, False))
+        mm("LN B32", "pL.n", [(T.pL[:, 128:136], T.LN[:, :], cs["B32"], False, True)], True)
+        tt("pL.n t8", "nx", cs["nx"], T.pL[:, 128:136], cs["t8"], A.max)
+        cp("nx", "nl", ul["nl"], cs["nx"])
+        zo = "zo%d" % v
+        if OPT["zs"]:
+            act("Y X nl", "Xn", T.Xn[:, :], ind(T.XW[:, 0:2176], ul["nl"]), scale=-1.0)
+            mm("Xn Ib Inh " + z, "pA.z", [(T.pA[:, 384:512], T.Inh[:, :], T[z][:, :], True, False),
+                                          (T.pA[:, 384:512], T.Ib[:, :], T.Xn[:, :], False, True)])
+            act("pA.z", "zs", T.zs[:, :], T.pA[:, 384:512], scale=-1.0, bias=-0.5)
+            act("zs", "zs", T.zs[:, :], T.zs[:, :], bias=M2)
+            act("zs", zo, T[zo][:, :], T.zs[:, :], bias=-M2)
+        else:
+            tt("Y X nl vz5", "zs", T.zs[:, :], ind(T.XW[:, 0:2176], ul["nl"]), T.vz5[:, :], A.add)
+            ts("zs", zo, T[zo][:, :], T.zs[:, :], M2, A.add, -M2, A.add)
+        if v == 0:
+            mm(MMall + " Bk", "pD1.x", [(T.pD1[:, h:128:16], T.MM1[:, ch(h, 128)], cs["Bk"], True, True) for h in range(16)], True)
+            act("pD1.x", "S0T", T.S0T[:, :], T.pD1[:, 0:128], bias=136.0)
+        if last:
+            act(zo, "w1", T.w1[:, :], T[zo][:, :], scale=0.5)
+            dma("Y", "w1", "", [(T.yz[:, :], T.w1[:, :])], 2.0)
+            break
+        send(zo, "z%d" % (v + 1), "aZ%d" % (v + 1))
+        act("nwin", "winb wn", T.winb[:, :], T.nwin[:, :], AF.Relu, scale=-1.0, bias=1.0, accum_out=cs["wn"])
+        act("wn At", "At", cs["At"], cs["At"], bias=cs["wn"])
+        act("At", "a1", cs["a1"], cs["At"], scale=1.0 / 128, bias=1.0 / 256 - 0.5)
+        act("a1", "a2", cs["a2"], cs["a1"], bias=M1)
+        act("a2", "a1", cs["a1"], cs["a2"], scale=-4194304.0, bias=M1 * 4194304.0)
+        act("a1 At", "Ac", cs["Ac"], cs["At"], scale=32768.0, bias=cs["a1"])
+
+        for q, b in enumerate(("pD0", "pD1", "pD0", "pD1")):
+            g1(q)
+            mm("Wg%d W1" % q, b + ".x", [(T[b][:, 0:32], T.W1[:, 15 - r:143 - r], T.Wg[:, 512 * q + r:512 * q + 512:16], r == 0, r == 15)
+                                         for r in range(16)])
+            ts(b + ".x", "Rl%d" % q, T.Rl[:, ch(q, 32)], T[b][:, 0:32], -1.0, A.mult, 2048.0, A.add)
+            piece(OPT["g2"][q], "X X2 pad Rl%d" % q, "XR", q, X2win, T.Rl)
+
+    mm("I32 S0T", "pE.VA", [(T.pE[:, 0:128], T.I32[:, :], T.S0T[:, :], True, False)], True)
+    for q in range(4):
+        g1(q)
+        act("TT " + R0l, "dead%d" % q, T.dead[:, ch(q)], ind(Twin, T.R0l[:, ch(q, 32)]), AF.Relu, scale=-1.0)
+        mm("Wg%d B16" % q, "pK.1", [(T.pK[:, h:128:16], T.Wg[:, ch(h, 128)], B16, True, True) for h in range(4 * q, 4 * q + 4)])
+        mm("dead%d Bkn" % q, "pE.VA", [(T.pE[:, h:128:16], T.dead[:, ch(h, 128)], cs["Bkn"], False, False) for h in range(4 * q, 4 * q + 4)], True)
+    shut("pE.VA", T.pE[:, 0:128])
+    vT = T.pK[:, 0:128]
+    tt("pK.1 MT", "sel", T.sel[:, :], vT, T.MT[:, :], A.is_equal)
+    ts("pK.1", "xx", T.xx[:, :], vT, 0.0, A.is_lt, -2049.0, A.mult)
+    act("pK.1", "za", T.za[:, :], vT, AF.Relu, scale=-1.0)
+    tt("pE.VA sel", "dz", T.dz[:, :], T.pE[:, 0:128], T.sel[:, :], A.mult)
+    act("pK.1", "hb", T.hb[:, :], vT, scale=-1.0, bias=2048.0)
+    mm("dz za I32", "pA.OT", [(T.pA[:, 0:128], T.za[:, :], T.I32[:, :], True, False), (T.pA[:, 0:128], T.dz[:, :], T.I32[:, :], False, True)], True)
+    mm("xx hb I32", "pB.u", [(T.pB[:, 0:128], T.xx[:, :], T.I32[:, :], True, False), (T.pB[:, 0:128], T.hb[:, :], T.I32[:, :], False, True)], True)
+    cp("pA.OT", "xn", T.xn[:, :], T.pA[:, 0:128])
+    dma("Y", "xn", "", [(T.yc[:, :], T.xn[:, :])], 2.0)
+    act("pB.u", "pf", T.pf[:, :], T.pB[:, 0:128])
+    dma("S", "pf", "", [(T.yr[:, :], T.pf[:, :])], 2.0)
+
+    Q = {"V": V, "S": S, "P": P, "G": g, "Y": g.sync}
+    cnt = {"V": 0, "S": 0, "P": 0, "G": 0}
+    known = {e: {} for e in Q}
+    lastw, readers, bank = {}, {}, {}
+    dmas, sent = [], 0
+
+    def need(e, evs):
+        kn = known[e]
+        for s, c, clk in sorted(evs, key=lambda x: -x[1]):
+            if kn.get(s, 0) < c:
+                Q[e].wait_ge(T.sem[s], c)
+                kn[s] = c
+                for s2, c2 in clk.items():
+                    if kn.get(s2, 0) < c2:
+                        kn[s2] = c2
+
+    if not ORDER:
+        ORDER.extend(arrange(ops))
+    for o in [ops[i] for i in ORDER[0]]:
+        e, r, w = o["e"], o["r"], o["w"]
+        if o["kind"] == "send":
+            w = []
+        evs = [ev for b in o["b"] for e2, ev in bank.get(b, {}).items() if e2 != e]
+        evs += [lastw[x] for x in r + w if x in lastw and "." not in x]
+        for x in w:
+            evs += readers.get(x, [])
+        need(e, evs)
+        if o["kind"] == "send":
+            src, dst, sem = o["fn"]
+            g.remote_dma(T[dst][:, :], T[src][:, :], T.sem[sem], T.sem.sent, pid, rid, emask)
+            sent += neng
+            lastw[dst] = (sem, neng, {})
+            continue
+        if o["kind"] == "dma":
+            s = "d%d" % len(dmas)
+            for dst, src in o["fn"]:
+                Q[e].dma_start(dst, src).then_inc(T.sem[s], 16)
+            ev = (s, 16 * len(o["fn"]), dict(known[e]))
+            dmas.append(ev)
+        else:
+            cnt[e] += 1
+            o["fn"]().then_inc(T.sem["s" + e], 1)
+            ev = ("s" + e, cnt[e], dict(known[e]))
+        for b in o["b"]:
+            bank.setdefault(b, {})[e] = ev
+        for x in r:
+            if "." not in x:
+                readers.setdefault(x, []).append(ev)
+        for x in w:
+            lastw[x] = ev
+            readers[x] = []
+    need("Y", dmas)
+    need("Y", [("s" + e, cnt[e], {}) for e in cnt])
+    g.wait_ge(T.sem.sent, sent)

@@ -10,47 +10,52 @@ def _sb(dtype, cols, names):
         SCRATCH[n] = ("sbuf", [128, cols], dtype)
 
 
-_sb(BF, 4240, "XW")
-_sb(BF, 2048, "XR OH Xg Ym ab")
-_sb(I32, 2048, "M0 R0B")
-_sb(F32, 2048, "MM1 io0 dead")
-_sb(F32, 2176, "TT")
-_sb(H, 2048, "Wg")
-_sb(BF, 512, "E32")
-_sb(BF, 576, "Ga Gb")
+_sb(BF, 4240, "ZX")
+_sb(F32, 4232, "IO")
+_sb(I32, 4104, "MX")
+_sb(F32, 2184, "TT")
+_sb(F32, 2048, "WT Mf")
+_sb(I32, 2048, "R0r")
+_sb(H, 2048, "Wg Tg MM OH")
+_sb(BF, 2048, "Xg Ym ab")
+_sb(BF, 2176, "Xm E16")
+_sb(BF, 1024, "eq")
+_sb(BF, 512, "E1 E3")
+_sb(F32, 256, "ta tb")
+_sb(H, 128, "z0 z1 z2 z3 zo0 zo1 zo2 zo3 zB")
 _sb(I32, 128, "Rin fin pi si qi")
-_sb(F32, 128, "Rf Rt Bt ones32 I32 rowA mask32 BB32 D1 rs1 MT diff d1 LP sel old vz5 dz za hb xx xn base "
-              "pf w0 w1 kc yy yS LN zs S0T OHo OLb m0")
-_sb(F32, 256, "SC")
-_sb(F32, 144, "D3 rs3 pm3 df3 d13 SC3 kS I136f")
-_sb(BF, 128, "BBu BBb Ib Inh Ih zin z0 z1 z2 z3 zo0 zo1 zo2 zo3 nzT nf nh emp nwin winb Xn nwB zero")
-_sb(H, 128, "BBh BB16 I16 rowA16 Of LM c0g Pv")
-_sb(BF, 144, "I136b Wb Wbn one5")
-_sb(H, 144, "SV Wn W1")
-_sb(U16, 128, "R0l Rl mu su f0 f1 f2 f3 fo0 fo1 fo2 ul")
-_sb(I32, 64, "it")
+_sb(F32, 128, "krow ones32 I32 Bt mask32 rs1 C0 O32 pf pm diff d1 d2 SCi SCo base LN yy sg sel dz w0 w1 xn xx")
+_sb(F32, 144, "rowA D3 rs3 pm3 SV")
+_sb(BF, 128, "Ib In BBn KC zero zin nf pen Xn Xc d2b")
+_sb(BF, 144, "W1 Wn Wp Wm RR tsp I136 one5 cw")
+_sb(H, 128, "k37 m0 idr cn za rv")
+_sb(U16, 128, "R0l R0m R0p c0l idL mu su f0 f1 f2 f3 fo0 fo1 fo2 ul")
+_sb(U16, 64, "dl")
+_sb(I32, 24, "it")
 _sb(F32, 128, "cs")
-_sb(BF, 16, "Bw")
-_sb(H, 32, "Bh")
+_sb(F32, 64, "q2")
+_sb(BF, 64, "Bq Bw")
 _sb(I32, 8, "th8")
-BANKS = "pD0 pD1 pK pA pB pC pE pL".split()
+BANKS = "pD0 pD1 pKA pKB pIA pIB pM pN".split()
 for _n in BANKS:
     SCRATCH[_n] = ("psum", [128, 512], F32)
 
 SEMAPHORES = (["sV", "sS", "sP", "sG", "sent"] + ["d%d" % i for i in range(24)]
-              + ["aF1", "aF2", "aF3", "aZ1", "aZ2", "aZ3"])
-M1 = 12582912.0
-M2 = 25165824.0
-CYC, GATH, SCAT, PECYC, HOP, FAR = 0.00104, 1.56, 3.8, 0.00053, 0.14, 2.6
-ROUNDS = 900
-OPT = {"g30": "VSSS", "g3": "VSVB", "g2": "SSSB", "g4": "SVSS", "zs": 1, "dz": 1, "base": 0, "lp": 1}
+              + ["a%s%d%d" % (x, v, h) for x in "fz" for v in range(1, VI) for h in range(2)])
+LN2 = 0.6931471805599453
+OFF = 28672.0
+BIG, MID = 2.0 ** 31, 2.0 ** 23
+CYC, GATH, SCAT, PECYC, HOP, FAR, FIRST = 0.00104, 1.56, 3.8, 0.00052, 0.10, 3.9, 2.0
+ROUNDS, SEED = 10000, 1
+OPT = {"x": ["SSSS", "SSSV", "SSSV", "SSSV"], "m": ["SSSS"] * 4, "w": ["", "S-SV", "S-SV", "S-SV"],
+       "t": (1, 1, 2), "r0": "S-V-", "xn": "S", "oh": "VVVV", "mm": "S", "parts": ["P-P-"] * 4, "early": 1, "gz": 0, "cut": 4, "cutc": 16, "wt": "VVVV", "end": (0, 8, 12, 14, 16), "zlate": (), "fsplit": (), "front": 1}
 ORDER = []
 
 
 def arrange(ops):
     n = len(ops)
     pred = [set() for _ in ops]
-    lastw, readers, lastp, users, closer = {}, {}, {}, {}, {}
+    lastw, readers, lastp, users, closer, queued = {}, {}, {}, {}, {}, set()
     for i, o in enumerate(ops):
         for x in o["r"] + o["w"]:
             if x in lastw:
@@ -68,14 +73,15 @@ def arrange(ops):
         else:
             for b in o["b"]:
                 users.setdefault(b, []).append(i)
-                assert not ops[lastp[b]]["open"]
+                assert not ops[lastp[b]]["open"], o["w"]
                 if closer.get(b) is not None:
                     pred[i].add(closer[b])
         if o["e"] == "P" and o["shut"]:
             closer[o["b"][0]] = i
         if o["e"] in "GY" or o["kind"] == "dma":
-            if o["e"] in lastp:
+            if o["e"] in lastp and lastp[o["e"]] not in pred[i]:
                 pred[i].add(lastp[o["e"]])
+                queued.add((lastp[o["e"]], i))
             lastp[o["e"]] = i
         for x in o["r"]:
             readers.setdefault(x, []).append(i)
@@ -89,63 +95,85 @@ def arrange(ops):
             succ[j].append(i)
 
     def gap(j, i):
-        same_queue = ops[j]["e"] == ops[i]["e"] and (ops[i]["e"] == "P" or (ops[j]["kind"] != "c" and ops[i]["kind"] != "c"))
+        same_queue = ops[j]["e"] == ops[i]["e"] == "P" or (j, i) in queued
         return ops[j]["c"] if same_queue else ops[j]["c"] + ops[j]["lat"]
 
     c = [o["c"] for o in ops]
     lat = [o["lat"] for o in ops]
-    fw = [[(j, gap(j, i)) for j in pred[i]] for i in range(n)]
-    bw = [[(i, c[i] + gap(j, i) - c[j]) for i in succ[j]] for j in range(n)]
+    fw = [[(i, gap(j, i)) for i in succ[j]] for j in range(n)]
+    bw = [[(j, c[i] + gap(j, i) - c[j]) for j in pred[i]] for i in range(n)]
 
     def place(key, back):
-        before, after = (bw, pred) if back else (fw, succ)
-        left = [len(x) for x in before]
-        cand = [i for i in range(n) if left[i] == 0]
-        at = [0.0] * n
+        after = bw if back else fw
+        left = [len(x) for x in (succ if back else pred)]
+        at = list(lat) if back else [0.0] * n
+        cand = [(key[i], i) for i in range(n) if not left[i]]
         busy = {x: [] for x in list("VSPGY") + BANKS}
         while cand:
-            i = min(cand, key=lambda x: key[x])
-            cand.remove(i)
-            e = ops[i]["e"]
-            t = max([at[j] + d for j, d in before[i]] + [lat[i] if back else 0.0])
-            lo, hi = (-lat[i], c[i]) if back else (0.0, c[i] + lat[i])
-            spans = [(a, b, 0.0, c[i]) for a, b, _ in busy[e] if b > t]
-            for x in ops[i]["b"]:
-                spans += [(a, b, lo, hi) for a, b, e2 in busy[x] if e2 != e and b > t + lo]
+            first = min(cand)
+            cand.remove(first)
+            i = first[1]
+            t, ci, e = at[i], c[i], ops[i]["e"]
+            q = busy[e]
+            lo, hi = (-lat[i], ci) if back else (0.0, ci + lat[i])
+            k = len(q)
+            while k and q[k - 1][1] > t + 1e-9:
+                k -= 1
             moved = True
             while moved:
+                while k < len(q) and q[k][0] < t + ci - 1e-9:
+                    t = max(t, q[k][1])
+                    k += 1
                 moved = False
-                for a, b, l, h in spans:
-                    if t + l < b - 1e-9 and t + h > a + 1e-9:
-                        t = b - l
-                        moved = True
+                for x in ops[i]["b"]:
+                    for a, b, e2 in reversed(busy[x]):
+                        if a < t - 3.0:
+                            break
+                        if e2 != e and t + lo < b - 1e-9 and t + hi > a + 1e-9:
+                            t = b - lo
+                            moved = True
             at[i] = t
-            busy[e].append((t, t + c[i], e))
+            q.insert(k, (t, t + ci))
             for x in ops[i]["b"]:
-                busy[x].append((t + lo, t + hi, e))
-            for j in after[i]:
+                u = busy[x]
+                k = len(u)
+                while k and u[k - 1][0] > t + lo:
+                    k -= 1
+                u.insert(k, (t + lo, t + hi, e))
+            for j, d in after[i]:
+                if at[j] < t + d:
+                    at[j] = t + d
                 left[j] -= 1
-                if left[j] == 0:
-                    cand.append(j)
+                if not left[j]:
+                    cand.append((key[j], j))
         return at
 
     prio = [0.0] * n
     for j in range(n - 1, -1, -1):
         prio[j] = max([gap(j, i) + prio[i] for i in succ[j]] + [c[j] + lat[j]])
-    best, seed = None, 1
+    visit = [sorted((i for i in range(n) if ops[i]["v"] == v), key=lambda i: ops[i]["w"][:1] != ["pm0"]) for v in range(VI)]
+    best, seed = None, SEED
     key = [-x for x in prio]
     for it in range(ROUNDS):
         at = place(key, False)
         span = max(at[i] + c[i] + lat[i] for i in range(n))
-        if best is None or span < best[0]:
+        if best is None or span <= best[0]:
             best = (span, at)
-        noise = []
         seed = (seed * 1103515245 + 12345) % 2147483648
         mid = seed / 2147483648.0 * best[0]
+        late = [-(best[1][i] + c[i]) for i in range(n)]
+        if it % 50 == 49:
+            a, b = 1 + seed // 64 % 3, 1 + (seed // 64 + 1 + seed // 1024 % 2) % 3
+            like = {ops[i]["role"]: late[i] - late[visit[a][0]] for i in visit[a]}
+            zero = late[visit[b][0]]
+            for i in visit[b]:
+                late[i] = like[ops[i]["role"]] + zero if ops[i]["role"] in like else late[i]
+            mid = -9.0
         for i in range(n):
-            seed = (seed * 1103515245 + 12345) % 2147483648
-            noise.append((seed / 2147483648.0 - 0.5) * (0.5, 1.5, 3.0)[it % 3] if abs(best[1][i] - mid) < 5.0 else 0.0)
-        back = place([-(best[1][i] + c[i]) + noise[i] for i in range(n)], True)
+            if abs(best[1][i] - mid) < 2.0:
+                seed = (seed * 1103515245 + 12345) % 2147483648
+                late[i] += (seed / 2147483648.0 - 0.5) * (0.3, 0.8, 2.0, 1.2)[it % 4]
+        back = place(late, True)
         key = [-(back[i] + c[i]) for i in range(n)]
     return sorted(range(n), key=lambda i: (best[1][i], i)), best[0]
 
@@ -162,6 +190,7 @@ def rank_program(g, core, T, topo):
     V, S, P = g.vector, g.scalar, g.tensor
     ops = []
     mark = [0]
+    seen, now = {}, [-1]
 
     def ind(win, off):
         mark[0] = 16 * off.shape[1]
@@ -170,39 +199,41 @@ def rank_program(g, core, T, topo):
     def add(e, r, w, kind, fn, c, lat=HOP):
         r, w = r.split(), w.split()
         b = sorted(set(x.split(".")[0] for x in r + w if "." in x))
-        ops.append({"e": e, "r": r, "w": w, "b": b, "kind": kind, "fn": fn, "c": c, "lat": lat})
+        role = (e, w[0][:1] + w[0][-1:] if w and w[0][:2] in ("fo", "zo", "f1", "f2", "f3", "z1", "z2", "z3") else "".join(w[:1]))
+        seen[role] = seen.get(role, 0) + 1
+        ops.append({"e": e, "r": r, "w": w, "b": b, "kind": kind, "fn": fn, "c": c, "lat": lat, "role": role + (seen[role],), "v": now[0]})
 
-    def op(e, r, w, fn, out, per=1.0, scat=False):
+    def op(e, r, w, fn, out, per=1.0, scat=False, more=0.0):
         n, mark[0] = mark[0], 0
-        cyc = n * (SCAT if scat else GATH) + 60 if n else max(64, out.shape[1] * per)
-        add(e, r, w, "c", fn, cyc * CYC + (0.17 if e == "G" else 0.03))
+        cyc = n * (SCAT if scat else GATH) + 70 if n else max(64, out.shape[1] * per)
+        add(e, r, w, "c", fn, cyc * CYC + (0.15 if e == "G" else 0.01) + more)
 
     def dma(e, r, w, pairs, lat):
         add(e, r, w, "dma", pairs, 0.06 * len(pairs), lat)
 
-    def send(src, dst, sem):
-        add("G", src, dst, "send", (src, dst, sem), 0.3, FAR)
+    def send(src, dst, h0, h1, lat):
+        add("G", names(src, h0, h1), names(dst, h0, h1), "send", (src, dst, slice(64 * h0, 64 * h1)), 0.3, lat)
 
     def tt(r, w, out, a, b, o, scat=False):
         op("V", r, w, lambda: V.tensor_tensor(out, a, b, o), out, 1.0 if "." in r else 2.0, scat)
 
-    def ts(r, w, out, a, s1, o0, s2=None, o1=None):
+    def ts(r, w, out, a, s1, o0, s2=None, o1=None, per=1.0):
         if o1 is None:
-            op("V", r, w, lambda: V.tensor_scalar(out, a, s1, None, o0), out)
+            op("V", r, w, lambda: V.tensor_scalar(out, a, s1, None, o0), out, per)
         else:
-            op("V", r, w, lambda: V.tensor_scalar(out, a, s1, s2, o0, o1), out)
+            op("V", r, w, lambda: V.tensor_scalar(out, a, s1, s2, o0, o1), out, per)
 
-    def cp(r, w, out, a, per=1.0):
-        op("V", r, w, lambda: V.tensor_copy(out, a), out, per)
+    def cp(r, w, out, a, scat=False):
+        op("V", r, w, lambda: V.tensor_copy(out, a), out, 1.0, scat)
 
-    def ms(w, out, c):
-        op("V", "", w, lambda: V.memset(out, c), out)
+    def ms(w, out, c, per=1.0):
+        op("V", "", w, lambda: V.memset(out, c), out, per)
 
     def scan(r, w, out, a, b, o0, o1):
         op("V", r, w, lambda: V.tensor_tensor_scan(out, a, b, 0.0, o0, o1), out)
 
-    def act(r, w, out, a, f=None, **kw):
-        op("S", r, w, lambda: S.activation(out, a, AF.Identity if f is None else f, **kw), out)
+    def act(r, w, out, a, f=None, more=0.0, **kw):
+        op("S", r, w, lambda: S.activation(out, a, AF.Identity if f is None else f, **kw), out, 1.0, False, more)
 
     def mm(r, w, lst, wide=()):
         def fn():
@@ -227,372 +258,416 @@ def rank_program(g, core, T, topo):
     def ch(q, n=512):
         return slice(n * q, n * q + n)
 
-    ul = {n: T.ul[:, 8 * i:8 * i + 8] for i, n in enumerate("bc bc3 cmp prm ol sl c0 nl".split())}
-    ul["e32"] = T.ul[:, 64:96]
-    cs = {}
-    o_ = 0
-    for n, k in (("p", 1), ("k", 1), ("k37", 1), ("kp", 1), ("k0", 1), ("v1", 1), ("v3", 1), ("Ac", 1), ("At", 1), ("wn", 1), ("p32", 1), ("a1", 1), ("a2", 1),
-                 ("t12", 2), ("tmp", 2), ("B32", 8), ("Bk", 8), ("Bkn", 8), ("al", 8), ("nw", 8), ("bias", 8), ("c0b", 8),
-                 ("nvl", 8), ("ix", 8), ("t8", 8), ("nx", 8)):
+    def names(x, a, b):
+        return " ".join("%s%d" % (x, q) for q in range(a, b + (b == 4 and x in ("Tg", "Wg"))))
+
+    ul, o_ = {}, 0
+    for n, k in (("dup", 16), ("pick", 8), ("pk2", 8), ("bcq", 8), ("bc3", 8), ("e1", 32), ("e3", 32)):
+        ul[n] = T.ul[:, o_:o_ + k]
+        o_ += k
+    for i, n in enumerate("idl ol idc cmpl sl nl".split()):
+        ul[n] = T.dl[:, 8 * i:8 * i + 8]
+    cs, o_ = {}, 0
+    for n, k in (("k", 1), ("p31", 1), ("p96", 1), ("c3", 1), ("p", 1), ("pk", 1), ("pk0", 1), ("pe", 1), ("p112", 1), ("kp", 1), ("k0", 1),
+                 ("t1c", 1), ("t2c", 1), ("t3c", 1), ("v3", 1), ("Ac", 1), ("sc", 1), ("kal", 1), ("t12", 2), ("a1", 1), ("a2", 1), ("t1s", 1), ("pad", 1),
+                 ("us", 8), ("cmpv", 8), ("B32", 8), ("t8", 8), ("al", 8), ("c1q", 8), ("nw", 8), ("ix", 8), ("tw", 8), ("fb", 8), ("nx", 8), ("th", 2)):
         cs[n] = T.cs[:, o_:o_ + k]
         o_ += k
-    th = T.cs[0:8, o_:o_ + 2]
-    Bw1, Bw3, B16, negb = T.Bw[:, 0:8], T.Bw[:, 8:16], T.Bh[:, 0:8], T.Bh[:, 16:24]
-    Xwin = T.XW[:, 128:2176]
-    X2win = T.XW[:, 128:4225]
-    Twin = T.TT[:, 0:2048]
-    r8 = T.rowA[:, 0:8]
+    th = cs["th"][0:8, :]
+    Bw3, Bb, Bk, Bkn, one_ = T.Bw[:, 0:8], T.Bw[:, 8:16], T.Bw[:, 16:24], T.Bw[:, 24:32], T.Bw[:, 32:40]
+    X0 = 2176
+    idwin, Xwin, Zout = T.ZX[:, 128:4225], T.ZX[:, X0:4225], T.ZX[:, 0:X0]
+    Y = T.Xm[:, 2048:2176]
+    Twin, Tout = T.TT[:, 128:2184], T.TT[:, 0:2176]
+    IOlo, IOall, IO32 = T.IO[:, 128:2328], T.IO[:, 128:4232], T.IO[:, 160:2208]
+    r8, ones = T.rowA[:, 0:8], T.one5[0:1, 0:128]
+    ends = slice(15, 128, 16)
 
-    def rin(a):
-        return (T.Rin[ch(a // 2, 32), ch(a % 2, 64)], T.rep[a, :])
+    ms("pad", T.ZX[:, X0:X0 + 16], -4096.0)
+    for q in range(0 if OPT["gz"] else 4):
+        ms("R0r%d" % q, T.R0r[:, ch(q)], 0)
+    dma("Y", "", "Rin", [(T.Rin[:, :], T.rep[:, :])], 2.0)
+    dma("S", "", "fin0 fin1", [(T.fin[:, :], T.fact[:, :])], 2.0)
+    dma("S", "", "zin th8", [(T.zin[:, :], T.z[:, :]), (T.th8[0:8, 0:2], T.thr[:, :])], 2.1)
+    dma("Y", "pad", "X pad", [(T.ZX[:, X0 + 1:4225], T.feat[:, :])], 4.0)
+    dma("Y", "", "M0", [(T.MX[:, 0:2048], T.memb[:, :])], 8.0)
+    dma("Y", "", "Z", [(T.ZX[:, 128:X0], T.feat[:, :])], 10.0)
 
-    dma("Y", "", "Rin", [rin(a) for a in range(0, 4)], 1.9)
-    dma("S", "", "Rin2 th8", [rin(a) for a in range(4, 8)] + [(T.th8[0:8, 0:2], T.thr[:, :])], 1.9)
-    dma("Y", "", "fin zin", [(T.fin[:, :], T.fact[:, :]), (T.zin[:, :], T.z[:, :])], 2.0)
-    ms("pad", T.XW[:, 2176:2192], 0.0)
-    dma("Y", "", "X", [(Xwin, T.feat[:, :])], 4.0)
-    dma("Y", "", "M0", [(T.M0[:, :], T.memb[:, :])], 8.0)
-    dma("Y", "", "R0B", [(T.R0B[i:128:16, :], T.rep[:, :]) for i in range(16)], 11.0)
-    dma("Y", "pad", "X2 pad", [(T.XW[:, 2177:4225], T.feat[:, :])], 13.0)
-
-    ms("ones32", T.ones32[:, :], 1.0)
-    ms("one5", T.one5[:, :], 1.0)
-    ms("zero", T.zero[:, :], 0.0)
     iota("it0", T.it[:, 0:1], [[0, 1]], 0, 1, False)
-    iota("it1", T.it[:, 8:16], [[16, 4], [64, 2]], 0, 0, False)
-    sel_("ones32", "I32", T.I32[:, :], T.ones32[:, :], [[-1, 128]], 0, 1)
-    iota("rowA", T.rowA[:, :], [[1, 128]], 0, 0)
+    iota("rowA", T.rowA[:, :], [[1, 144]], 0, 0)
+    iota("q2a", T.q2[:, 0:16], [[16, 8], [0, 2]], 0, 0)
+    iota("q2b", T.q2[:, 16:48], [[16, 2], [0, 16]], 0, 0)
+    iota("krow", T.krow[:, :], [[0, 8], [1, 16]], 0, 0)
+    act("rowA", "ones32", T.ones32[:, :], T.rowA[:, 0:128], scale=0.0, bias=1.0)
+    act("rowA", "one5", T.one5[:, :], T.rowA[:, :], scale=0.0, bias=1.0)
     sel_("ones32", "Bt", T.Bt[0:8, :], T.ones32[0:8, :], [[1, 8], [0, 16]], 0, -1)
-    iota("pi", T.pi[:, :], [[1, 128]], 128, -1, False)
-    sel_("one5", "I136b", T.I136b[:, 0:136], T.one5[:, 0:136], [[16, 8], [1, 17]], -1, -1)
-    iota("io0", T.io0[:, :], [[1, 2048]], 0, 0)
-    iota("TT", T.TT[:, :], [[-1, 2176]], 2048, 0)
-    iota("MT", T.MT[:, :], [[0, 8], [-128, 16]], 2048, -1)
+    sel_("one5", "I136", T.I136[:, 0:136], T.one5[:, 0:136], [[16, 8], [1, 17]], -1, -1)
+    if OPT["gz"]:
+        iota(names("R0r", 0, 4), T.R0r[:, :], [[0, 2048]], 0, 0, False)
+    dma("Y", names("R0r", 0, 4), "R0r " + names("R0r", 0, 4), [(T.R0r[0:128:16, :], T.rep[:, :])], 4.0)
+    for q, (a, b) in enumerate(((0, 640), (640, 1152), (1152, 1664), (1664, 2328))):
+        iota("IO%d" % q, T.IO[:, a:b], [[1, b - a]], a - 128, 0)
+    iota("zero", T.zero[:, :], [[0, 128]], 0, 0)
+    iota("pen", T.pen[:, :], [[0, 128]], 0, 0)
+    iota("tsp", T.tsp[:, :], [[0, 144]], 0, 0)
+    iota("Wn", T.Wn[:, :], [[0, 144]], 0, 0)
+    iota("SV", T.SV[:, 0:136], [[0, 136]], 0, 16)
+    op("G", "SV", "SV", lambda: g.iota(T.SV[:, 0:136:17], [[0, 8]], 2048, 1, allow_small_or_imprecise_dtypes=True), r8, 2.0)
+    op("G", "zero", "RR", lambda: g.affine_select(T.RR[:, 0:128], T.zero[:, :], [[-1, 128]], A.not_equal, -MID, 0, 1), T.zero[:, :], 2.0)
+    iota("RR2", T.RR[:, 128:144], [[0, 16]], -2 ** 19, 0)
 
-    cp("it0", "p", cs["p"], T.it[:, 0:1])
-    ts("it0", "it2", T.it[:, 1:2], T.it[:, 0:1], 15, A.bitwise_and)
-    cp("it2", "k", cs["k"], T.it[:, 1:2])
-    ts("it0", "it3", T.it[:, 2:3], T.it[:, 0:1], 96, A.bitwise_and)
-    cp("it3", "p32", cs["p32"], T.it[:, 2:3])
-    ts("it1 k", "prm", ul["prm"], T.it[:, 8:16], cs["k"], A.add)
-    ts("rowA p32", "e32", ul["e32"], T.rowA[:, 0:32], cs["p32"], A.add)
-    mm("Bt", "pA.OT", [(T.pA[:, 0:128], T.Bt[0:8, :], T.Bt[0:8, :], True, True)], True)
-    cp("th8", "th", th, T.th8[0:8, 0:2])
-    mm("Bt th", "pC.ol", [(T.pC[:, 0:2], T.Bt[0:8, :], th, True, True)], True)
-    act("pA.OT", "BB32", T.BB32[:, :], T.pA[:, 0:128])
-    act("pC.ol", "t12", cs["t12"], T.pC[:, 0:2])
-    cp("Rin Rin2 prm", "Rf", T.Rf[:, :], ind(T.Rin[:, :], ul["prm"]))
-    op("V", "Rf", "Rt", lambda: V.transpose(T.Rt[:, :], T.Rf[:, :]), T.Rt[:, :])
-    for q in range(4):
-        cp("Rt", "R0l%d" % q, T.R0l[:, q:128:4], T.Rt[:, ch(q, 32)])
-    R0l = "R0l0 R0l1 R0l2 R0l3"
-    cp("fin", "f0", T.f0[:, :], T.fin[:, :])
-    act("zin", "z0", T.z0[:, :], T.zin[:, :], scale=2.0)
-    act("I32", "Inh", T.Inh[:, :], T.I32[:, :], scale=-0.5)
-    act("I32", "Ib", T.Ib[:, :], T.I32[:, :])
-    act("Ib e32", "E32", T.E32[:, :], ind(T.Ib[:, :], ul["e32"]))
-    B_ = T.BB32[:, 0:128:16]
-    act("BB32", "Bw1", Bw1, B_, scale=32768.0)
-    cp("I32", "I16", T.I16[:, :], T.I32[:, :])
-    act("t12", "tmp", cs["tmp"][:, 0:1], cs["t12"][:, 0:1], scale=-32768.0, bias=-1024.0)
-    act("k tmp", "v1", cs["v1"], cs["k"], scale=-2048.0, bias=cs["tmp"][:, 0:1])
-    act("I32 v1", "D1", T.D1[:, :], T.I32[:, :], scale=cs["v1"])
-    ms("rs1", T.rs1[:, :], 0.0)
-    ms("rs1", T.rs1[:, 0:128:16], -1e12)
-    ts("pi", "si", T.si[:, :], T.pi[:, :], 15, A.bitwise_and)
-    ts("si", "mask32", T.mask32[:, :], T.si[:, :], 0.0, A.is_equal)
-    cp("BB32", "B16", B16, B_)
-    ts("rowA", "bc", ul["bc"], r8, 16.0, A.mult, 15.0, A.add)
-    act("BB32", "B32", cs["B32"], B_)
-    act("BB32", "Bw3", Bw3, B_, scale=262144.0)
-    act("BB32", "BBu", T.BBu[:, :], T.BB32[:, :], scale=1.0 / 64)
-    act("BB32", "BBb", T.BBb[:, :], T.BB32[:, :])
-    act("I32", "Ih", T.Ih[:, :], T.I32[:, :], scale=-32768.0)
-    act("k", "k37", cs["k37"], cs["k"], scale=37.0, bias=-31.0 / 64)
+    def upper():
+        iota("IO4", T.IO[:, 2328:3280], [[1, 952]], 2200, 0)
+        iota("IO5", T.IO[:, 3280:4232], [[1, 952]], 3152, 0)
+
+    if not OPT["gz"]:
+        upper()
+    lo, hi = names("IO", 0, 4), names("IO", 0, 6)
+    dma("Y", lo, "TT", [(T.TT[:, 128:2184], T.IO[:, 129:2185])], 8.0)
+
+    for i, (s1, o0) in enumerate(((15, A.bitwise_and), (31, A.bitwise_and), (96, A.bitwise_and))):
+        ts("it0", "it%d" % (i + 1), T.it[:, i + 1:i + 2], T.it[:, 0:1], s1, o0)
+    ts("it0", "it4", T.it[:, 4:5], T.it[:, 0:1], 3, A.arith_shift_right, 1, A.bitwise_and)
+    cp("it1 it2 it3 it4", "k p31 p96 c3", T.cs[:, 0:4], T.it[:, 1:5])
+    ts("q2a k", "dup", ul["dup"], T.q2[:, 0:16], cs["k"], A.add)
+    ts("rowA p31", "pick", ul["pick"], r8, 32.0, A.mult, cs["p31"], A.add)
+
+    def turn(r, src, w, dst, lst, plus=0.0):
+        cp(r + " dup", "ta", T.ta[:, :], ind(src, ul["dup"]))
+        op("V", "ta", "tb", lambda: V.transpose(T.tb[:, :], T.ta[:, :]), T.tb[:, :])
+        ts("tb " + lst, w, dst, ind(T.tb[:, :], ul[lst]), plus, A.add)
+
+    act("p96 p31", "p", cs["p"], cs["p96"], bias=cs["p31"])
+    act("p96 k", "pe", cs["pe"], cs["p96"], bias=cs["k"])
+    act("p k", "p112", cs["p112"], cs["k"], scale=-1.0, bias=cs["p"])
+    act("k p31", "pk0", cs["pk0"], cs["k"], scale=31.0, bias=cs["p31"])
+    act("c3 pk0", "pk", cs["pk"], cs["c3"], scale=-255.0, bias=cs["pk0"])
     act("k", "kp", cs["kp"], cs["k"], bias=1.0)
-    ts("k", "k0", cs["k0"], cs["k"], 0.0, A.is_equal, -1.0, A.mult)
-    act("kp BB32", "Bk", cs["Bk"], B_, scale=cs["kp"])
-    act("Bk", "Bkn", cs["Bkn"], cs["Bk"], scale=-1.0)
-    ts("BB32", "BBh", T.BBh[:, :], T.BB32[:, :], 256.0, A.mult)
-    ts("BB32", "BB16", T.BB16[:, :], T.BB32[:, :], -1.0, A.mult)
-    cp("rowA", "rowA16", T.rowA16[:, :], T.rowA[:, :])
-    act("rowA k", "t8", cs["t8"], r8, scale=16.0, bias=cs["k"])
-    act("t8", "al", cs["al"], cs["t8"], bias=2048.0)
-    ts("t8", "negb", negb, cs["t8"], -1.0, A.mult, -64.0, A.add)
+    act("k", "kal", cs["kal"], cs["k"], bias=OFF - 128)
+    ts("rowA p", "I32", T.I32[:, :], T.rowA[:, 0:128], cs["p"], A.is_equal)
+    ts("rowA p112", "B32", cs["B32"], T.rowA[:, 0:128:16], cs["p112"], A.is_equal)
+    ts("q2b pe", "e1", ul["e1"], T.q2[:, 16:48], cs["pe"], A.add)
+    ts("rowA p96", "e3", ul["e3"], T.rowA[:, 0:32], cs["p96"], A.add)
+    ts("rowA pk", "pk2", ul["pk2"], r8, 2.0, A.mult, cs["pk"], A.add)
+    cp("rowA", "bcq", ul["bcq"], r8)
     ts("rowA", "bc3", ul["bc3"], r8, 17.0, A.mult, 16.0, A.add)
-    ts("rowA kp", "cmp", ul["cmp"], r8, 17.0, A.mult, cs["kp"], A.add)
-    ms("Wb", T.Wb[:, :], 0.0)
-    act("BB32", "Wb", T.Wb[:, 15:143:16], B_, scale=256.0)
-    act("Wb", "Wbn", T.Wbn[:, :], T.Wb[:, :], scale=-1.0)
-    ts("Wb", "Wn", T.Wn[:, :], T.Wb[:, :], -1.0, A.mult)
-    ts("Wb", "W1", T.W1[:, :], T.Wb[:, :], 1.0 / 256, A.mult)
-    ms("I136b", T.I136b[:, 0:136:17], 0.0)
-    act("I136b", "I136f", T.I136f[:, 0:136], T.I136b[:, 0:136])
-    act("t12", "tmp2", cs["tmp"][:, 1:2], cs["t12"][:, 1:2], scale=-262144.0, bias=-16384.0 * 15.5)
-    act("k tmp2", "v3", cs["v3"], cs["k"], scale=16384.0, bias=cs["tmp"][:, 1:2])
-    act("I136b v3", "D3", T.D3[:, 0:136], T.I136b[:, 0:136], scale=cs["v3"])
-    act("I136b", "I136b", T.I136b[:, 0:136], T.I136b[:, 0:136], scale=2147483648.0)
-    ms("SV", T.SV[:, 0:136], 128.0)
-    ts("p ones32", "SV", T.SV[:, 0:136:17], T.ones32[:, 0:8], cs["p"], A.mult)
-    ms("rs3", T.rs3[:, :], 0.0)
-    ms("rs3", T.rs3[:, 0:136:17], 1e12)
-    ms("Ac", cs["Ac"], 0.0)
-    ms("At", cs["At"], 0.0)
+    ts("krow k", "mask32", T.mask32[:, :], T.krow[:, :], cs["k"], A.is_equal)
+    for n, s in (("Ib", 1.0), ("In", -1.0)):
+        act("I32", n, T[n][:, :], T.I32[:, :], scale=s)
+    act("rowA", "W1", T.W1[:, :], T.rowA[:, :], scale=0.0)
+    for n, s in (("Wn", -2048.0), ("W1", 1.0)):
+        act("B32", n, T[n][:, 15:143:16], cs["B32"], scale=s)
+    act("In e1", "E1", T.E1[:, :], ind(T.In[:, :], ul["e1"]))
+    act("In e3", "E3", T.E3[:, :], ind(T.In[:, :], ul["e3"]))
+    cp("th8", "th", th, T.th8[0:8, 0:2])
+    mm("Bt th", "pM.t", [(T.pM[:, 40:42], T.Bt[0:8, :], th, True, True)], True)
+    act("pM.t", "t12", cs["t12"], T.pM[:, 40:42])
+    act("t12", "t1c", cs["t1c"], cs["t12"][:, 0:1], scale=2.0 ** 30)
+    act("t12", "t1s", cs["t1s"], cs["t12"][:, 0:1], scale=-2.0 ** 20, bias=-63.5 * 2 ** 20)
+    act("t12", "Ac", cs["Ac"], cs["t12"][:, 0:1], scale=2.0 ** 20)
+    act("krow", "KC", T.KC[0:1, :], T.krow[0:1, :], scale=-65536.0, bias=-32768.0)
+    act("krow", "rs1", T.rs1[:, :], T.krow[:, :], scale=2e18, bias=-1e18)
+    act("krow", "k37", T.k37[0:1, :], T.krow[0:1, :], scale=1184.0)
+    act("t12", "t2c", cs["t2c"], cs["t12"][:, 1:2], bias=0.5)
+    act("t12 k", "v3", cs["v3"], cs["t12"][:, 1:2], scale=-4096.0, bias=cs["k"])
+    act("I136", "I136", T.I136[:, 0:136:17], T.I136[:, 0:136:17], scale=0.0)
+    act("I136 v3", "D3", T.D3[:, 0:136], T.I136[:, 0:136], scale=cs["v3"])
+    act("B32", "D3", T.D3[:, 0:136:17], cs["B32"], scale=-MID / 16)
+    act("B32", "Bw3", Bw3, cs["B32"], scale=4096.0)
+    act("SV", "rs3", T.rs3[:, 0:136], T.SV[:, 0:136], scale=1e17, bias=-2040e17)
+    mm("ones32 D3 I32 SV", "pN.c", [(T.pN[:, 0:136], T.ones32[:, :], T.D3[:, 0:136], True, False),
+                                    (T.pN[:, 0:136], T.I32[:, :], T.SV[:, 0:136], False, True)], True)
+    act("pN.c", "SV", T.SV[:, 0:136], T.pN[:, 0:136])
+    mm("Bt", "pN.c", [(T.pN[:, 0:128], T.Bt[0:8, :], T.Bt[0:8, :], True, True)], True)
+    act("pN.c", "BBn", T.BBn[:, :], T.pN[:, 0:128], scale=-2048.0)
+    act("mask32", "E16a", T.E16[:, 0:128], T.mask32[:, :])
+    dma("Y", "E16a one5", "E16", [(T.E16[:, ch(j, 128)], T.E16[:, 0:128] if j < 16 else T.one5[:, 0:128]) for j in range(1, 17)], 6.0)
+    act("ones32", "cw", T.cw[0:1, 0:8], T.ones32[0:1, 0:8], scale=-MID)
+    act("ones32", "cw", T.cw[0:1, 8:9], T.ones32[0:1, 0:1], scale=0.0)
+    act("rowA k", "t8", cs["t8"], r8, scale=16.0, bias=cs["k"])
+    act("rowA kal", "al", cs["al"], r8, scale=16.0, bias=cs["kal"])
+    act("t8", "c1q", cs["c1q"], cs["t8"], AF.Exp, 1.3, scale=-LN2, bias=63 * LN2)
+    act("p c1q", "sc", cs["sc"], cs["p"], AF.Exp, scale=LN2, bias=-64 * LN2)
+    for q in range(8):
+        act("B32 c1q", "Bq%d" % q, T.Bq[:, ch(q, 8)], cs["B32"], scale=cs["c1q"][:, q:q + 1])
 
-    XRall = "XR0 XR1 XR2 XR3 XR0h XR1h XR2h XR3h"
-    MMall = "MM0 MM1 MM2 MM3"
-    OHall = "OH0 OH1 OH2 OH3"
+    def diag(out, Wd, src, first, stop):
+        return [(out, Wd[:, 15 - r:143 - r], src[:, r:src.shape[1]:16], first and r == 0, stop and r == 15) for r in range(16)]
 
-    def gather(e, r, w, out, src):
+    def gather(e, r, w, out, src, **kw):
         if e == "V":
             cp(r, w, out, src)
         else:
-            act(r, w, out, src)
+            act(r, w, out, src, **kw)
 
-    def piece(e, r, dst, q, win, lst):
-        w = "%s%d" % (dst, q)
-        if e == "B":
-            gather("V", r, w, T[dst][:, ch(2 * q, 256)], ind(win, lst[:, ch(2 * q, 16)]))
-            gather("S", r, w + "h", T[dst][:, ch(2 * q + 1, 256)], ind(win, lst[:, ch(2 * q + 1, 16)]))
-        else:
-            gather(e, r, w + " " + w + "h", T[dst][:, ch(q)], ind(win, lst[:, ch(q, 32)]))
+    def diff_abs(src, q, E, zA, zn, zlate):
+        b = ("pD0", "pD1")[q % 2]
+        two = [(zn + " " + E, zA[ch(q, 32), :], T[E][ch(q, 32), :]), ("%s%d Ib" % (src, q), T.Ib[:, :], T[src][:, ch(q)])]
+        for i, (r, l, rh) in enumerate(two[::-1] if zlate else two):
+            mm(r, b + ".x", [(T[b][:, :], l, rh, i == 0, i == 1)])
+        s = 2.0 ** 20 if E == "E1" else 1.0
+        act(b + ".x", "ab%d" % q, T.ab[:, ch(q)], T[b][:, :], AF.Abs, scale=s, bias=1024.0 * s)
 
-    def diff_mm(src, q, b):
-        mm("nzT E32", b + ".x", [(T[b][:, :], T.nzT[ch(q, 32), :], T.E32[ch(q, 32), :], True, False)])
-        mm("%s%d %s%dh Ib" % (src, q, src, q), b + ".x", [(T[b][:, :], T.Ib[:, :], T[src][:, ch(q)], False, True)])
+    PI, PK = ("pIA", "pIB"), ("pKA", "pKB")
+    PARTS = {1: ((0, 2),), 2: ((0, 1), (1, 2))}
 
-    def absp(q, b):
-        act(b + ".x", "ab%d" % q, T.ab[:, ch(q)], T[b][:, :], AF.Abs)
+    def pieces(s):
+        cut = [q for q in range(4) if s[q] != "-"] + [4]
+        return [(a, b, s[a]) for a, b in zip(cut, cut[1:])]
 
-    def sum_mm(q, reg, first, step, Bw, name):
-        mm("ab%d %s" % (q, name), reg, [(T.pK[ch(q, 32), first + k:first + k + 7 * step + 1:step], T.ab[:, 512 * q + k:512 * q + 512:16], Bw,
-                                         False, False) for k in range(16)])
+    def tables():
+        turn("Rin", T.Rin[:, :], "R0p", T.R0p[:, :], "pk2", 1.0)
+        turn("fin0 fin1", T.fin[:, :], "f00 f01", T.f0[:, :], "pick")
+        ts("R0p", "R0l", T.R0l[:, :], T.R0p[:, :], -1.0, A.add, per=0.5)
+        ts("R0l", "R0m", T.R0m[:, :], T.R0l[:, :], -1.0, A.mult, 4096.0, A.add, 0.5)
+        for a, b, _ in pieces(OPT["oh"]):
+            c, l = slice(512 * a, 512 * b), slice(32 * a, 32 * b)
+            tt("M0 R0l " + names("IO", a, b), names("OH", a, b), T.OH[:, c], ind(T.MX[:, 0:2048], T.R0l[:, l]), T.IO[:, 128 + 512 * a:128 + 512 * b], A.is_equal)
 
-    def shut(reg, out):
-        mm("zero Ib", reg, [(out, T.Ib[:, :], T.zero[:, :], False, True)])
+    def table_W():
+        if OPT["gz"]:
+            upper()
+        for a, b, e in pieces(OPT["wt"]):
+            c, l = slice(512 * a, 512 * b), slice(32 * a, 32 * b)
+            tt("R0m %s %s" % (names("OH", a, b), hi), names("WT", a, b), T.WT[:, c], ind(IOall, T.R0m[:, l]), T.OH[:, c], A.mult)
 
-    def diag(out, Wd, src, first, stop):
-        return [(out, Wd[:, 15 - r:143 - r], src[:, r:128:16], first and r == 0, stop and r == 15) for r in range(16)]
-
-    def g1(q):
-        tt("TT %s OH%d" % (R0l, q), "Wg%d" % q, T.Wg[:, ch(q)], ind(Twin, T.R0l[:, ch(q, 32)]), T.OH[:, ch(q)], A.mult)
-
-    DB = ("pD0", "pD1")
-    for q, e in ((0, "V"), (2, "S"), (1, "V"), (3, "S")):
-        gather(e, "X " + R0l, "XR%d" % q, T.XR[:, ch(q)], ind(Xwin, T.R0l[:, ch(q, 32)]))
-    for q in range(4):
-        cp("M0 " + R0l, "MM%d" % q, T.MM1[:, ch(q)], ind(T.M0[:, :], T.R0l[:, ch(q, 32)]))
-    for q in range(8):
-        tt("M0 io0 " + R0l, "OH%d" % (q // 2), T.OH[:, ch(q, 256)], ind(T.M0[:, :], T.R0l[:, ch(q, 16)]), T.io0[:, ch(q, 256)], A.is_equal)
+    mm("zin Ib", "pM.a", [(T.pM[:, 256:384], T.zin[:, :], T.Ib[:, :], True, True)])
+    act("pM.a", "z00 z01", T.z0[:, :], T.pM[:, 256:384], bias=1024.0)
+    tables()
 
     for v in range(VI):
         f, z = "f%d" % v, "z%d" % v
+        zB, fa, za_ = T.zB[:, :], names(f, 0, 2), "zB"
+        zA, zn = T[z], names(z, 0, 2)
         last = v == VI - 1
-        cp(f, "Of", T.Of[:, :], T[f][:, :], 0.5)
-        mm("Of I16", "pA.OT", [(T.pA[:, 0:128], T.Of[:, :], T.I16[:, :], True, True)])
-        mm(z + " Inh", "pB.z", [(T.pB[:, 384:512], T[z][:, :], T.Inh[:, :], True, True)])
-        act("pB.z", "nzT", T.nzT[:, :], T.pB[:, 384:512])
-        mm("ones32 D1", "pK.1", [(T.pK[:, 0:128], T.ones32[:, :], T.D1[:, :], True, False)], True)
-        mm(z + " BBu", "pB.u", [(T.pB[:, 0:128], T.BBu[:, :], T[z][:, :], True, True)])
-        tt("Of pB.u", "pf", T.pf[:, :], T.Of[:, :], T.pB[:, 0:128], A.mult)
-        act(z, "vz5", T.vz5[:, :], T[z][:, :], scale=0.5, bias=-0.5)
-        act("pf k37", "w0", T.w0[:, :], T.pf[:, :], bias=cs["k37"])
-        act("w0", "w1", T.w1[:, :], T.w0[:, :], bias=M1)
-
-        for q, e in enumerate(OPT["g30"] if v == 0 else OPT["g3"]):
-            piece(e, XRall + " " + f, "Xg", q, T.XR[:, :], T[f])
-            diff_mm("Xg", q, DB[q % 2])
-            absp(q, DB[q % 2])
-            sum_mm(q, "pK.1", 0, 16, Bw1, "Bw1")
-        shut("pK.1", T.pK[:, 0:128])
-
-        key = T.pK[:, 0:128]
-        scan("pK.1 rs1", "pm", T.SC[:, 0:128], T.rs1[:, :], key, A.add, A.max)
-        tt("pm pK.1", "diff", T.diff[:, :], T.SC[:, 0:128], key, A.subtract)
-        tt("pA.OT diff", "d1", T.d1[:, :], T.pA[:, 0:128], T.diff[:, :], A.subtract)
-        act("pK.1", "nf", T.nf[:, :], key, AF.Relu, scale=-1.0)
-        scan("diff d1", "os", T.SC[:, 128:256], T.diff[:, :], T.d1[:, :], A.min, A.max)
-        tt("os bc mask32", "LM", T.LM[:, :], ind(T.SC[:, 128:256], ul["bc"]), T.mask32[:, :], A.mult)
-        mm("LM B16", "pC.ol", [(T.pC[:, 0:8], T.LM[:, :], B16, True, True)])
-        act("os bc", "OLb", T.OLb[:, :], ind(T.SC[:, 128:256], ul["bc"]), bias=32.0)
-        mm("OLb I32", "pE.oB", [(T.pE[:, 384:512], T.OLb[:, :], T.I32[:, :], True, True)], True)
-        cp("pC.ol", "ol", ul["ol"], T.pC[:, 0:8])
-        act("pE.oB", "sel", T.sel[:, :], T.pE[:, 384:512])
-        ts(MMall + " ol", "mu", T.mu[:, :], ind(T.MM1[:, :], ul["ol"]), 0.0, A.max)
-        act(MMall + " ol", "m0", T.m0[:, :], ind(T.MM1[:, :], ul["ol"]))
-        tt(MMall + " ol sel", "pi", T.pi[:, :], ind(T.MM1[:, :], ul["ol"]), T.sel[:, :], A.mult)
-        ts("pi", "si", T.si[:, :], T.pi[:, :], 5, A.arith_shift_right, 2047, A.bitwise_and)
-        cp("si", "su", T.su[:, :], T.si[:, :])
-
-        mm("nf Ih w1 I32 Of I16", "pB.f", [(T.pB[:, 128:256], T.I32[:, :], T.w1[:, :], True, False),
-                                           (T.pB[:, 128:256], T.I16[:, :], T.Of[:, :], False, False),
-                                           (T.pB[:, 128:256], T.nf[:, :], T.Ih[:, :], False, True)], (0,))
-        tt("pB.f Of", "qi", T.qi[:, :], T.pB[:, 128:256], T.Of[:, :], A.max)
-        ts("qi", "fin", T.fin[:, :], T.qi[:, :], 2047, A.bitwise_and)
-        if last:
-            cp("fin", "w0", T.w0[:, :], T.fin[:, :])
-            dma("Y", "w0", "", [(T.yo[:, :], T.w0[:, :])], 2.0)
+        seen.clear()
+        now[0] = v
+        if v:
+            mm(zn + " Ib", "pM.a", [(T.pM[:, 256:384], zA[:, :], T.Ib[:, :], True, True)])
+            act("pM.a", "zB", zB, T.pM[:, 256:384])
         else:
-            cp("fin", "fo%d" % v, T["fo%d" % v][:, :], T.fin[:, :])
-            send("fo%d" % v, "f%d" % (v + 1), "aF%d" % (v + 1))
+            act("zin", "zB", zB, T.zin[:, :], bias=1024.0)
+        if v:
+            for q0, q1, e in pieces(OPT["w"][v]):
+                src, r = ind(T.WT[:, :], T[f][:, 32 * q0:32 * q1]), names("WT", 0, 4) + " " + names(f, q0 // 2, (q1 + 1) // 2)
+                if e == "S":
+                    act(r, names("Wg", q0, q1), T.Wg[:, 512 * q0:512 * q1], src, scale=1.0 / 2048, bias=-1.0)
+                else:
+                    ts(r, names("Wg", q0, q1), T.Wg[:, 512 * q0:512 * q1], src, 1.0 / 2048, A.mult, -1.0, A.add)
+            for h in range(2):
+                for j in range(0, 16, OPT["cutc"]):
+                    mm(names("Wg", 2 * h, 2 * h + 2) + " Wn", PI[h] + ".c",
+                       diag(T[PI[h]][:, 64:128], T.Wn, T.Wg[:, ch(h, 1024)], True, True)[j:j + OPT["cutc"]])
+                ts(PI[h] + ".c", "c0l%d" % h, T.c0l[:, ch(h, 64)], T[PI[h]][:, 64:128], -OFF, A.add)
+        q0 = 0
+        for n in OPT["t"] if v else ():
+            h, cols, lst = q0 // 2, slice(512 * q0, 512 * (q0 + n)), slice(32 * q0, 32 * (q0 + n))
+            w = names("Tg", q0, q0 + n)
+            tt("TT c0l%d %s" % (h, names("Wg", q0, q0 + n)), w, T.Tg[:, cols], ind(Twin, T.c0l[:, lst]), T.Wg[:, cols], A.min)
+            out = T[PI[h]][:, 32 * (q0 % 2):32 * (q0 % 2 + n)]
+            reg = " ".join("%s.i%d" % (PI[h], q) for q in range(q0, q0 + n))
+            mm(w + " Wn", reg, diag(out, T.Wn, T.Tg[:, cols], True, True))
+            ts(reg, names("idL", q0, q0 + n), T.idL[:, lst], out, -OFF, A.add)
+            q0 += n
+        for q0, q1, e in pieces(OPT["r0"]) if v == 0 else ():
+            gather(e, "X pad R0p", names("Ym", q0, q1), T.Ym[:, 512 * q0:512 * q1], ind(Xwin, T.R0p[:, 32 * q0:32 * q1]))
+        if v and OPT["early"]:
+            tt("yy base sl", "TT", ind(Tout, ul["sl"]), T.yy[:, :], T.base[:, :], A.max, True)
+        ts(fa, "O32", T.O32[:, :], T[f][:, :], 32.0, A.mult)
+        for h in range(2):
+            mm("I32 O32", PI[h] + ".o", [(T[PI[h]][:, 384:448], T.I32[:, :], T.O32[:, ch(h, 64)], True, True)], True)
+        for j in range(0, 16, OPT["cut"]):
+            mm(za_ + " W1", "pM.u", diag(T.pM[:, 0:8], T.W1, zB, True, True)[j:j + OPT["cut"]])
+        act("pM.u", "us", cs["us"], T.pM[:, 0:8], scale=1.0 / 32, bias=-511.0)
+        tt("us bcq O32", "pf", T.pf[:, :], ind(cs["us"], ul["bcq"]), T.O32[:, :], A.mult)
 
-        cp("R0B ol", "c0g", T.c0g[:, :], ind(T.R0B[:, :], ul["ol"]))
-        mm("c0g Wn", "pC.c0", diag(T.pC[:, 24:32], T.Wn, T.c0g, True, True))
-        ts("pC.c0", "c0", ul["c0"], T.pC[:, 24:32], -1.0 / 4096, A.mult)
-        act("pC.c0", "c0b", cs["c0b"], T.pC[:, 24:32], scale=-1.0 / 4096)
-        if v == 0:
-            ts("c0g k0", "Pv", T.Pv[:, :], T.c0g[:, :], -2048.0, A.add, cs["k0"], A.mult)
-        else:
-            act(OHall + " ol", "OHo", T.OHo[:, :], ind(T.OH[:, :], ul["ol"]))
-            tt("TT c0 OHo", "Pv", T.Pv[:, :], ind(Twin, ul["c0"]), T.OHo[:, :], A.mult)
-        act("TT c0", "old", T.old[:, :], ind(Twin, ul["c0"]))
-        mm("Pv BB16 old I32", "pL.vB", [(T.pL[:, 256:384], T.BB16[:, :], T.Pv[:, :], True, False),
-                                        (T.pL[:, 256:384], T.I32[:, :], T.old[:, :], False, True)], (1,))
-        act("pL.vB", "nh", T.nh[:, :], T.pL[:, 256:384], AF.Abs)
-        mm("Pv BBh I16 rowA16", "pE.VA", [(T.pE[:, 0:128], T.I16[:, :], T.rowA16[:, :], True, False),
-                                          (T.pE[:, 0:128], T.BBh[:, :], T.Pv[:, :], False, True)])
-        act("m0", "emp", T.emp[:, :], T.m0[:, :], AF.Relu, scale=-1.0)
-        if OPT["lp"]:
-            act("pm bc", "LP", T.LP[:, :], ind(T.SC[:, 0:128], ul["bc"]))
-            mm("LP I32", "pE.pm", [(T.pE[:, 128:256], T.LP[:, :], T.I32[:, :], True, True)], True)
-            act("pE.pm Ac", "nwB", T.nwB[:, :], T.pE[:, 128:256], AF.Relu, scale=-1.0, bias=cs["Ac"])
-            mm("nwB Wbn", "pC.v", diag(T.pC[:, 16:24], T.Wbn, T.nwB, True, False))
-            mm("Pv Wn I16 negb", "pC.v", [(T.pC[:, 16:24], T.I16[:, :], negb, False, False)] + diag(T.pC[:, 16:24], T.Wn, T.Pv, False, True))
-            act("pC.v", "bias", cs["bias"], T.pC[:, 16:24])
-        else:
-            tt("pm bc mask32", "LP", T.LP[:, :], ind(T.SC[:, 0:128], ul["bc"]), T.mask32[:, :], A.mult)
-            mm("LP B32", "pC.pm", [(T.pC[:, 8:16], T.LP[:, :], cs["B32"], True, True)], True)
-            mm("Pv Wn I16 negb", "pC.v", [(T.pC[:, 16:24], T.I16[:, :], negb, True, False)] + diag(T.pC[:, 16:24], T.Wn, T.Pv, False, True))
-            ts("pC.pm Ac", "nw", cs["nw"], T.pC[:, 8:16], cs["Ac"], A.is_le, -4194304.0, A.mult)
-            tt("pC.v nw", "bias", cs["bias"], T.pC[:, 16:24], cs["nw"], A.add)
-        act("pC.v", "nvl", cs["nvl"], T.pC[:, 16:24], AF.Relu, scale=64.0)
-
-        mm("ones32 D3", "pK.3", [(T.pK[:, 128:264], T.ones32[:, :], T.D3[:, 0:136], True, False)], True)
-        for q in range(4):
-            piece(OPT["g4"][q], "X mu", "Xg", q, Xwin, T.mu)
-            tt("X su Xg%d Xg%dh" % (q, q), "Ym%d" % q, T.Ym[:, ch(q)], ind(Xwin, T.su[:, ch(q, 32)]), T.Xg[:, ch(q)], A.min)
-            diff_mm("Ym", q, DB[q % 2])
-            absp(q, DB[q % 2])
-            if q == 3:
-                mm("emp I136b", "pK.3", [(T.pK[:, 128:264], T.emp[:, :], T.I136b[:, 0:136], False, False)])
-            sum_mm(q, "pK.3", 129, 17, Bw3, "Bw3")
-        mm("nh I136b", "pK.3", [(T.pK[:, 128:264], T.nh[:, :], T.I136b[:, 0:136], False, True)])
-        mm("m0 I136f I16 SV", "pA.val", [(T.pA[:, 128:264], T.m0[:, :], T.I136f[:, 0:136], True, False),
-                                         (T.pA[:, 128:264], T.I16[:, :], T.SV[:, 0:136], False, True)], (0,))
-
-        off = [0]
-        for q in range(8):
-            off.append(off[-1] + 128 - 16 * q)
-        for q in range(8):
-            act("pE.VA bias", "Ga%d" % q, T.Ga[:, off[q]:off[q + 1]], T.pE[:, 16 * q:128], AF.Abs, bias=cs["bias"][:, q:q + 1])
-        act(" ".join("Ga%d" % q for q in range(8)), "Gb", T.Gb[:, :], T.Ga[:, :], AF.Relu, scale=-1.0, bias=65.0)
-        mm("Gb BBb zero", "pE.cnt", [(T.pE[:, 256:384], T.BBb[:, :], T.zero[:, :], True, False)]
-           + [(T.pE[:, 256 + 16 * q:384], T.BBb[:, :], T.Gb[:, off[q]:off[q + 1]], False, q == 0) for q in range(7, -1, -1)])
-        act("pE.cnt", "nwin", T.nwin[:, :], T.pE[:, 256:384], AF.Abs, bias=-1.0)
-        mm("c0b nvl I32 nwin Wb", "pC.R2",
-           [(T.pC[:, 32:40], T.I32[:, :], cs["c0b"], True, False), (T.pC[:, 32:40], T.I32[:, :], cs["nvl"], False, False)]
-           + diag(T.pC[:, 32:40], T.Wb, T.nwin, False, True), (0, 1))
-        tt("pC.R2 al", "ix", cs["ix"], T.pC[:, 32:40], cs["al"], A.min)
-        cp("ix", "sl", ul["sl"], cs["ix"])
-
-        if OPT["dz"]:
-            act(XRall + " ol", "Xn", T.Xn[:, :], ind(T.XR[:, :], ul["ol"]))
-            mm("Xn Ib Inh " + z, "pA.z", [(T.pA[:, 384:512], T.Inh[:, :], T[z][:, :], True, False),
-                                          (T.pA[:, 384:512], T.Ib[:, :], T.Xn[:, :], False, True)])
-            act("pA.z", "Xn", T.Xn[:, :], T.pA[:, 384:512], AF.Abs, scale=2.0)
-            mm("Xn Ib Inh " + z, "pA.z", [(T.pA[:, 384:512], T.Inh[:, :], T[z][:, :], True, False),
-                                          (T.pA[:, 384:512], T.Ib[:, :], T.Xn[:, :], False, True)])
-            act("pA.z", "Y", T.XW[:, 0:128], T.pA[:, 384:512], bias=0.5)
-        else:
-            tt(XRall + " ol vz5", "dz", T.dz[:, :], ind(T.XR[:, :], ul["ol"]), T.vz5[:, :], A.subtract)
-            act("dz", "za", T.za[:, :], T.dz[:, :], AF.Abs, scale=2.0, bias=-1.0)
-            tt("za vz5", "Y", T.XW[:, 0:128], T.za[:, :], T.vz5[:, :], A.subtract)
-        if OPT["base"]:
-            mm("old m0 I32 nh Ih", "pL.b", [(T.pL[:, 384:512], T.I32[:, :], T.old[:, :], True, False),
-                                            (T.pL[:, 384:512], T.I32[:, :], T.m0[:, :], False, False),
-                                            (T.pL[:, 384:512], T.Ih[:, :], T.nh[:, :], False, True)], (0, 1))
-            act("pL.b", "xx", T.xx[:, :], T.pL[:, 384:512], AF.Relu, bias=1.0)
-            if OPT["base"] == 1:
-                act("xx", "xn", T.xn[:, :], T.xx[:, :], scale=-1.0)
-                mm("old xn I32", "pL.b", [(T.pL[:, 384:512], T.I32[:, :], T.old[:, :], True, False),
-                                          (T.pL[:, 384:512], T.I32[:, :], T.xn[:, :], False, True)], True)
-                act("pL.b", "base", T.base[:, :], T.pL[:, 384:512])
+        for q0, q1, e in pieces(OPT["x"][v]):
+            if v:
+                r, src = "Z X pad " + names("idL", q0, q1), ind(idwin, T.idL[:, 32 * q0:32 * q1])
             else:
-                tt("old xx", "base", T.base[:, :], T.old[:, :], T.xx[:, :], A.subtract)
-        else:
-            act("nh", "hb", T.hb[:, :], T.nh[:, :], scale=-8192.0, bias=4096.0)
-            tt(MMall + " ol hb", "xx", T.xx[:, :], ind(T.MM1[:, :], ul["ol"]), T.hb[:, :], A.min)
-            act("xx", "xn", T.xn[:, :], T.xx[:, :], scale=-1.0, bias=-1.0)
-            tt("TT c0 xn", "base", T.base[:, :], ind(Twin, ul["c0"]), T.xn[:, :], A.min)
+                r, src = names("Ym", 0, 4) + " " + fa, ind(T.Ym[:, :], T.f0[:, 32 * q0:32 * q1])
+            gather(e, r, names("Xg", q0, q1), T.Xg[:, 512 * q0:512 * q1], src)
+        for p, (q0, q1, _) in enumerate(pieces(OPT["parts"][v])):
+            for q in range(q0, q1):
+                diff_abs("Xg", q, "E1", zA, zn, v > 0 and q in OPT["zlate"])
+            h, c, c4, e4 = q0 // 2, slice(32 * q0, 32 * q1), slice(2 * q0, 2 * q1), slice(32 * q0 + 15, 32 * q1, 16)
+            qn = lambda x: names(x, q0, q1)
+            key, kn, i0, n = T[PK[p % 2]][:, c], "%s.k%d" % (PK[p % 2], p), 32 * (q0 % 2), 32 * (q1 - q0)
+            mm(qn("ab") + " W1 one5 KC", kn, [(key, ones, T.KC[0:1, c], True, False)] + diag(key, T.W1, T.ab[:, 512 * q0:512 * q1], False, True))
+            scan(kn + " rs1", qn("pm"), T.pm[:, c], T.rs1[:, c], key, A.min, A.max)
+            tt(kn + " " + qn("pm"), qn("diff"), T.diff[:, c], T.pm[:, c], key, A.subtract)
+            tt(PI[h] + ".o " + qn("diff"), qn("d2"), T.d2[:, c], T[PI[h]][:, 384 + i0:384 + i0 + n], T.diff[:, c], A.subtract)
+            scan(qn("diff") + " " + qn("d2"), qn("SCo"), T.SCo[:, c], T.diff[:, c], T.d2[:, c], A.min, A.max)
+            ts(qn("SCo"), qn("ol"), ul["ol"][:, c4], T.SCo[:, e4], 1.0 / 32, A.mult)
+            if v:
+                tt(qn(PI[h] + ".i") + " " + qn("diff"), qn("d1"), T.d1[:, c], T[PI[h]][:, i0:i0 + n], T.diff[:, c], A.subtract)
+                scan(qn("diff") + " " + qn("d1"), qn("SCi"), T.SCi[:, c], T.diff[:, c], T.d1[:, c], A.min, A.max)
+                ts(qn("SCi"), qn("idl"), ul["idl"][:, c4], T.SCi[:, e4], -OFF, A.add)
+            else:
+                reg, row, out = qn(PI[h] + ".i"), T.Tg[:, 512 * q0:512 * q0 + n], T[PI[h]][:, i0:i0 + n // 16]
+                cp("R0r " + qn("ol"), qn("Tg"), row, ind(T.R0r[:, :], ul["ol"][:, c4]))
+                mm(qn("Tg") + " W1", reg, diag(out, T.W1, row, True, True))
+                cp(reg, qn("idl"), ul["idl"][:, c4], out)
+                act(reg, qn("SCi"), T.SCi[:, e4], out, bias=OFF)
+            Mwin, mn = (T.MX[:, :], "M0 M1 ") if v else (T.MX[:, 0:2048], "M0 ")
+            ts(mn + qn("idl"), qn("mu"), T.mu[:, c], ind(Mwin, ul["idl"][:, c4]), 1.0, A.add)
+            ts(qn("mu"), qn("m0"), T.m0[:, c], T.mu[:, c], -1.0, A.add)
+            tt("%s %s %s" % (lo, qn("ol"), qn("m0")), qn("pi"), T.pi[:, c], ind(IO32, ul["ol"][:, c4]), T.m0[:, c], A.mult)
+            ts(qn("pi"), qn("si"), T.si[:, c], T.pi[:, c], 5, A.arith_shift_right, 2047, A.bitwise_and)
+            ts(qn("si"), qn("su"), T.su[:, c], T.si[:, c], 1.0, A.add)
+            act(kn + " t1c", qn("nf"), T.nf[:, c], key, AF.Relu, scale=-1024.0, bias=cs["t1c"])
+        SCi, pm, m0, idl = (names(x, 0, 4) for x in ("SCi", "pm", "m0", "idl"))
 
-        key3 = T.pK[:, 128:264]
-        scan("pK.3 rs3", "pm3", T.pm3[:, 0:136], T.rs3[:, 0:136], key3, A.add, A.min)
-        tt("pm3 pK.3", "df3", T.df3[:, 0:136], key3, T.pm3[:, 0:136], A.subtract)
-        act("pK.3", "kS", T.kS[:, 0:136], key3)
-        tt("pA.val df3", "d13", T.d13[:, 0:136], T.pA[:, 128:264], T.df3[:, 0:136], A.subtract)
-        act("kS cmp", "kc", T.kc[:, :], ind(T.kS[:, 0:136], ul["cmp"]))
-        scan("df3 d13", "SC3", T.SC3[:, 0:136], T.df3[:, 0:136], T.d13[:, 0:136], A.min, A.max)
-        tt("SC3 bc3 kc", "yy", T.yy[:, :], ind(T.SC3[:, 0:136], ul["bc3"]), T.kc[:, :], A.max)
-        mm("yy I32", "pB.y", [(T.pB[:, 256:384], T.yy[:, :], T.I32[:, :], True, True)], True)
-        act("pB.y", "yS", T.yS[:, :], T.pB[:, 256:384], scale=-1.0, bias=2176.0)
-        tt("yS base sl", "TT", ind(T.TT[:, :], ul["sl"]), T.yS[:, :], T.base[:, :], A.max, True)
-        tt("SC3 bc3 mask32", "LN", T.LN[:, :], ind(T.SC3[:, 0:136], ul["bc3"]), T.mask32[:, :], A.mult)
-        mm("nwin Wbn", "pL.n", diag(T.pL[:, 128:136], T.Wbn, T.nwin, True, False))
-        mm("LN B32", "pL.n", [(T.pL[:, 128:136], T.LN[:, :], cs["B32"], False, True)], True)
-        tt("pL.n t8", "nx", cs["nx"], T.pL[:, 128:136], cs["t8"], A.max)
-        cp("nx", "nl", ul["nl"], cs["nx"])
-        zo = "zo%d" % v
-        if OPT["zs"]:
-            act("Y X nl", "Xn", T.Xn[:, :], ind(T.XW[:, 0:2176], ul["nl"]), scale=-1.0)
-            mm("Xn Ib Inh " + z, "pA.z", [(T.pA[:, 384:512], T.Inh[:, :], T[z][:, :], True, False),
-                                          (T.pA[:, 384:512], T.Ib[:, :], T.Xn[:, :], False, True)])
-            act("pA.z", "zs", T.zs[:, :], T.pA[:, 384:512], scale=-1.0, bias=-0.5)
-            act("zs", "zs", T.zs[:, :], T.zs[:, :], bias=M2)
-            act("zs", zo, T[zo][:, :], T.zs[:, :], bias=-M2)
-        else:
-            tt("Y X nl vz5", "zs", T.zs[:, :], ind(T.XW[:, 0:2176], ul["nl"]), T.vz5[:, :], A.add)
-            ts("zs", zo, T[zo][:, :], T.zs[:, :], M2, A.add, -M2, A.add)
-        if v == 0:
-            mm(MMall + " Bk", "pD1.x", [(T.pD1[:, h:128:16], T.MM1[:, ch(h, 128)], cs["Bk"], True, True) for h in range(16)], True)
-            act("pD1.x", "S0T", T.S0T[:, :], T.pD1[:, 0:128], bias=136.0)
+        for h0, h1 in ((0, 1), (1, 2)) if v in OPT["fsplit"] else ((0, 2),):
+            c, out = slice(64 * h0, 64 * h1), T.pM[:, 128 + 64 * h0:128 + 64 * h1]
+            mm("I32 pf one5 k37 In " + names("nf", 2 * h0, 2 * h1), "pM.f", [(out, T.I32[:, :], T.pf[:, c], True, False),
+                                                                     (out, ones, T.k37[0:1, c], False, False),
+                                                                     (out, T.In[:, :], T.nf[:, c], False, True)], (0,))
+            tt("pM.f O32", "qi", T.qi[:, c], out, T.O32[:, c], A.max)
+            ts("qi", names("fin", h0, h1), T.fin[:, c], T.qi[:, c], 5, A.arith_shift_right, 2047, A.bitwise_and)
+            if not last:
+                cp(names("fin", h0, h1), names("fo%d" % v, h0, h1), T["fo%d" % v][:, c], T.fin[:, c])
+                send("fo%d" % v, "f%d" % (v + 1), h0, h1, FAR + (FIRST if v == h0 == 0 else 0.0))
         if last:
-            act(zo, "w1", T.w1[:, :], T[zo][:, :], scale=0.5)
+            turn("fin0 fin1", T.fin[:, :], "w0", T.w0[:, :], "pick")
+            dma("Y", "w0", "", [(T.yo[:, :], T.w0[:, :])], 2.0)
+
+        if v == 0:
+            table_W()
+        idv = T.SCi[:, ends]
+        if v:
+            ts(SCi, "idc", ul["idc"], idv, -OFF, A.add, 2048.0, A.min)
+            act("TT idc", "pen", T.pen[:, :], ind(Twin, ul["idc"]), AF.Relu, scale=-2 * BIG, bias=BIG)
+            act("Z X pad " + idl, "Xc", T.Xc[:, :], ind(idwin, ul["idl"]))
+        else:
+            act("Z " + idl, "Xc", T.Xc[:, :], ind(T.ZX[:, 128:X0], ul["idl"]))
+        act(m0, "base", T.base[:, :], T.m0[:, :], scale=-1.0 / 2048, bias=-1.0 / 2048)
+        y_ = T.pN[:, 256:384]
+        mm("Xc Ib In " + za_, "pN.b", [(y_, T.In[:, :], zB, True, False), (y_, T.Ib[:, :], T.Xc[:, :], False, True)])
+        act("pN.b", "d2b", T.d2b[:, :], y_, AF.Abs, scale=2.0, bias=2048.0)
+        mm("d2b Ib In " + za_, "pN.b", [(y_, T.In[:, :], zB, True, False), (y_, T.Ib[:, :], T.d2b[:, :], False, True)])
+        act("pN.b", "Y", Y, y_, bias=1024.5)
+
+        act(pm + " Ac", "nw", cs["nw"], T.pm[:, ends], AF.Relu, scale=-1.0, bias=cs["Ac"])
+        tt(SCi + " nw", "cmpv", cs["cmpv"], idv, cs["nw"], A.add)
+        ts("cmpv", "cmpl", ul["cmpl"], cs["cmpv"], OFF + (4100 if v else 2100), A.min, -OFF, A.add)
+        act("cmpl " + (hi if v else lo), "idr", T.idr[:, :], ind(IOall if v else IOlo, ul["cmpl"]), bias=-2048.0)
+        a0 = [64 * (q // 4) for q in range(8)]
+        for q in range(8):
+            ts("idr cmpv", "eq%d" % q, T.eq[:, 128 * q + a0[q]:128 * q + 128], T.idr[:, a0[q]:128], OFF + 2048, A.add,
+               cs["cmpv"][:, q:q + 1], A.is_equal, 0.75)
+        mm(names("eq", 0, 8) + " " + names("Bq", 0, 8), "pM.v",
+           [(T.pM[a0[q]:128, 8:16], T.eq[:, 128 * q + a0[q]:128 * q + 128], T.Bq[:, ch(q, 8)], q == 0, q == 1) for q in (0, 4, 5, 6, 7, 2, 3, 1)])
+        act("pM.v sc", "tw", cs["tw"], T.pM[:, 8:16], AF.Abs, scale=cs["sc"], bias=-0.75)
+        act("tw", "tsp", T.tsp[:, 15:143:16], cs["tw"], AF.Sign, bias=-0.5)
+        act(SCi, "one_", one_, idv, AF.Relu, scale=2.0 ** 20, bias=-2.0 ** 20 * (OFF + 2047.5))
+        out = T.pM[:, 16:25]
+        mm("one5 cw I32 In one_ " + SCi, "pM.w", [(out, ones, T.cw[0:1, 0:9], True, False), (T.pM[:, 16:24], T.I32[:, :], idv, False, False),
+                                                  (T.pM[:, 16:24], T.In[:, :], one_, False, False)], (1,))
+        mm("tsp RR RR2", "pM.w", diag(out, T.tsp, T.RR, False, True))
+        tt("pM.w al", "ix", cs["ix"], T.pM[:, 16:24], cs["al"], A.max)
+        ts("ix", "sl", ul["sl"], cs["ix"], 128 - OFF, A.add)
+        if not last:
+            act("pM.w Ac", "a1", cs["a1"], T.pM[:, 24:25], bias=cs["Ac"])
+            act("a1 t1s", "a2", cs["a2"], cs["a1"], AF.Sign, bias=cs["t1s"])
+            act("a1 a2", "Ac", cs["Ac"], cs["a2"], scale=-2.0 ** 26, bias=cs["a1"])
+
+
+        zo = "zo%d" % v
+        for q0, q1, e in pieces(OPT["m"][v]):
+            gather(e, "X pad " + names("mu", q0, q1), names("Xm", q0, q1), T.Xm[:, 512 * q0:512 * q1],
+                   ind(Xwin, T.mu[:, 32 * q0:32 * q1]))
+        key3, kn = T.pKA[:, 128:264], "pKA.3"
+        mm("I32 SV", kn, [(key3, T.I32[:, :], T.SV[:, 0:136], True, False)], True)
+        for q in range(4):
+            h = q // 2
+            tt("X pad su%d Xm%d" % (q, q), "Ym%d" % q, T.Ym[:, ch(q)], ind(Xwin, T.su[:, ch(q, 32)]), T.Xm[:, ch(q)], A.min)
+            diff_abs("Ym", q, "E3", zA, zn, False)
+            if q == 3:
+                mm("tsp RR", kn, [(T.pKA[:, 128:264:17], T.RR[:, 0:128], T.tsp[:, 15:143:16], False, False)])
+            mm("ab%d Bw3" % q, kn, [(T.pKA[ch(q, 32), 129 + k:129 + k + 7 * 17 + 1:17], T.ab[:, 512 * q + k:512 * q + 512:16], Bw3,
+                                     False, False) for k in range(16)])
+            if q == 3:
+                mm("pen I136", kn, [(key3, T.pen[:, :], T.I136[:, 0:136], False, True)])
+            if q % 2:
+                eb = T.pKB[:, 256 + 64 * h:320 + 64 * h]
+                if h == 0:
+                    mm("Ib zero", "pKB.e", [(T.pKB[:, 256:384], T.Ib[:, :], T.zero[:, :], True, False)])
+                for j in range(0, 16, OPT["cut"]):
+                    mm(names("ab", q - 1, q + 1) + " W1", "pKB.e", diag(eb, T.W1, T.ab[:, ch(h, 1024)], False, False)[j:j + OPT["cut"]])
+        mm("Ib pen", "pKB.e", [(T.pKB[:, 256:384], T.Ib[:, :], T.pen[:, :], False, True)])
+        act("pKB.e t2c", "sg", T.sg[:, :], T.pKB[:, 256:384], AF.Sign, scale=-1.0, bias=cs["t2c"])
+        early = OPT["early"] and not last
+        if early:
+            tt("sg base sl", "TT", ind(Tout, ul["sl"]), T.sg[:, :], T.base[:, :], A.max, True)
+        pm3 = T.pm3[:, 0:136]
+        scan(kn + " rs3", "pm3", pm3, T.rs3[:, 0:136], key3, A.max, A.min)
+        tt("pm3 bc3 mask32", "LN", T.LN[:, :], ind(pm3, ul["bc3"]), T.mask32[:, :], A.mult)
+        out = T.pN[:, 144:152]
+        mm("LN B32", "pN.n", [(out, T.LN[:, :], cs["B32"], True, True)], True)
+        cp("pN.n", "n1", T.it[:, 8:16], out)
+        ts("n1", "n2", T.it[:, 16:24], T.it[:, 8:16], 4095, A.bitwise_and)
+        cp("n2", "nl", ul["nl"], T.it[:, 16:24])
+        gather(OPT["xn"], names("Xm", 0, 4) + " Y nl", "Xn", T.Xn[:, :], ind(T.Xm[:, :], ul["nl"]))
+        out = T.pN[:, 384:512]
+        if last:
+            mm("Xn Ib zB", "pN.z", [(out, T.Ib[:, :], zB, True, False), (out, T.Ib[:, :], T.Xn[:, :], False, True)])
+        else:
+            mm("Xn Ib " + zn, "pN.z", [(out, T.Ib[:, :], zA[:, :], True, False), (out, T.Xn[:, :], T.Ib[:, :], False, True)])
+        act("pN.z", names(zo, 0, 2), T[zo][:, :], out, scale=0.5, bias=511.75)
+        tt("E16 nl base", "cn", T.cn[:, :], ind(T.E16[:, :], ul["nl"]), T.base[:, :], A.mult)
+        mm("BBn cn", "pN.c", [(T.pN[:, 0:128], T.BBn[:, :], T.cn[:, :], True, True)])
+        tt("pN.c sg", "yy", T.yy[:, :], T.pN[:, 0:128], T.sg[:, :], A.mult)
+        if not early:
+            tt("yy base sl", "TT", ind(Tout, ul["sl"]), T.yy[:, :], T.base[:, :], A.max, True)
+        if not last:
+            send(zo, "z%d" % (v + 1), 0, 2, FAR)
+            cp("Xn sl", "Z", ind(Zout, ul["sl"]), T.Xn[:, :], True)
+        if v == 0:
+            iota("M1", T.MX[:, 2048:4104], [[1, 2056]], -1, 0, False)
+            iota("Wp", T.Wp[:, :], [[0, 144]], 0, 0)
+            iota("Wm", T.Wm[:, :], [[0, 144]], 0, 0)
+            act("B32 kp", "Wp", T.Wp[:, 15:143:16], cs["B32"], scale=cs["kp"])
+            act("Wp", "Wm", T.Wm[:, 15:143:16], T.Wp[:, 15:143:16], scale=-1.0)
+            act("k", "pk0", cs["pk0"], cs["k"], scale=128.0)
+            act("rowA pk0", "C0", T.C0[:, :], T.rowA[:, 0:128], bias=cs["pk0"])
+        if last:
+            act(names(zo, 0, 2), "w1", T.w1[:, :], T[zo][:, :], bias=-1024.0)
             dma("Y", "w1", "", [(T.yz[:, :], T.w1[:, :])], 2.0)
-            break
-        send(zo, "z%d" % (v + 1), "aZ%d" % (v + 1))
-        act("nwin", "winb wn", T.winb[:, :], T.nwin[:, :], AF.Relu, scale=-1.0, bias=1.0, accum_out=cs["wn"])
-        act("wn At", "At", cs["At"], cs["At"], bias=cs["wn"])
-        act("At", "a1", cs["a1"], cs["At"], scale=1.0 / 128, bias=1.0 / 256 - 0.5)
-        act("a1", "a2", cs["a2"], cs["a1"], bias=M1)
-        act("a2", "a1", cs["a1"], cs["a2"], scale=-4194304.0, bias=M1 * 4194304.0)
-        act("a1 At", "Ac", cs["Ac"], cs["At"], scale=32768.0, bias=cs["a1"])
 
-        for q, b in enumerate(("pD0", "pD1", "pD0", "pD1")):
-            g1(q)
-            mm("Wg%d W1" % q, b + ".x", [(T[b][:, 0:32], T.W1[:, 15 - r:143 - r], T.Wg[:, 512 * q + r:512 * q + 512:16], r == 0, r == 15)
-                                         for r in range(16)])
-            ts(b + ".x", "Rl%d" % q, T.Rl[:, ch(q, 32)], T[b][:, 0:32], -1.0, A.mult, 2048.0, A.add)
-            piece(OPT["g2"][q], "X X2 pad Rl%d" % q, "XR", q, X2win, T.Rl)
-
-    mm("I32 S0T", "pE.VA", [(T.pE[:, 0:128], T.I32[:, :], T.S0T[:, :], True, False)], True)
+    now[0] = VI
     for q in range(4):
-        g1(q)
-        act("TT " + R0l, "dead%d" % q, T.dead[:, ch(q)], ind(Twin, T.R0l[:, ch(q, 32)]), AF.Relu, scale=-1.0)
-        mm("Wg%d B16" % q, "pK.1", [(T.pK[:, h:128:16], T.Wg[:, ch(h, 128)], B16, True, True) for h in range(4 * q, 4 * q + 4)])
-        mm("dead%d Bkn" % q, "pE.VA", [(T.pE[:, h:128:16], T.dead[:, ch(h, 128)], cs["Bkn"], False, False) for h in range(4 * q, 4 * q + 4)], True)
-    shut("pE.VA", T.pE[:, 0:128])
-    vT = T.pK[:, 0:128]
-    tt("pK.1 MT", "sel", T.sel[:, :], vT, T.MT[:, :], A.is_equal)
-    ts("pK.1", "xx", T.xx[:, :], vT, 0.0, A.is_lt, -2049.0, A.mult)
-    act("pK.1", "za", T.za[:, :], vT, AF.Relu, scale=-1.0)
-    tt("pE.VA sel", "dz", T.dz[:, :], T.pE[:, 0:128], T.sel[:, :], A.mult)
-    act("pK.1", "hb", T.hb[:, :], vT, scale=-1.0, bias=2048.0)
-    mm("dz za I32", "pA.OT", [(T.pA[:, 0:128], T.za[:, :], T.I32[:, :], True, False), (T.pA[:, 0:128], T.dz[:, :], T.I32[:, :], False, True)], True)
-    mm("xx hb I32", "pB.u", [(T.pB[:, 0:128], T.xx[:, :], T.I32[:, :], True, False), (T.pB[:, 0:128], T.hb[:, :], T.I32[:, :], False, True)], True)
-    cp("pA.OT", "xn", T.xn[:, :], T.pA[:, 0:128])
+        if OPT["mm"] == "S":
+            cp("M0", "Mf%d" % q, T.Mf[:, ch(q)], T.MX[:, ch(q)])
+    for q in range(4):
+        if OPT["mm"] == "S":
+            act(names("Mf", 0, 4) + " R0l", "MM%d" % q, T.MM[:, ch(q)], ind(T.Mf[:, :], T.R0l[:, ch(q, 32)]), bias=1.0)
+        else:
+            ts("M0 R0l", "MM%d" % q, T.MM[:, ch(q)], ind(T.MX[:, 0:2048], T.R0l[:, ch(q, 32)]), 1.0, A.add)
+    vT, sT = T.pIA[:, 128:256], T.pIB[:, 128:256]
+
+    def rows(out, Wd, src, h0, h1, first, stop):
+        return [(out, Wd[:, 15 - h:143 - h], src[:, ch(h, 128)], first and h == h0, stop and h == h1 - 1) for h in range(h0, h1)]
+
+    mm(names("MM", 0, 4) + " Wp", "pIB.s", rows(sT, T.Wp, T.MM, 0, 16, True, False))
+    mm("In one5", "pIA.v", [(vT, T.In[:, :], T.one5[:, 0:128], True, False)])
+    cut = OPT["end"]
+    for a, b in zip(cut, cut[1:]):
+        part = [h // 4 if h < 14 else 4 for h in range(a, b)]
+        c, l = slice(128 * a, 128 * b), slice(8 * a, 8 * b)
+        tg, wg = (" ".join("%s%d" % (x, q) for q in sorted(set(part))) for x in ("Tg", "Wg"))
+        tt("TT R0l " + names("OH", 0, 4), tg, T.Tg[:, c], ind(Twin, T.R0l[:, l]), T.OH[:, c], A.mult)
+        act("TT R0l", wg, T.Wg[:, c], ind(Twin, T.R0l[:, l]), AF.Relu, scale=-2048.0)
+        mm(tg + " W1", "pIA.v", rows(vT, T.W1, T.Tg, a, b, False, b == 16))
+        mm(wg + " Wm", "pIB.s", rows(sT, T.Wm, T.Wg, a, b, False, b == 16))
+    tt("pIA.v C0", "sel", T.sel[:, :], vT, T.C0[:, :], A.is_equal)
+    act("pIA.v", "za", T.za[:, :], vT, AF.Relu, scale=-2048.0, bias=-2048.0)
+    tt("pIB.s sel", "dz", T.dz[:, :], sT, T.sel[:, :], A.mult)
+    act("za", "rv", T.rv[:, :], T.za[:, :], bias=-1.0)
+    tt("dz za", "xn", T.xn[:, :], T.dz[:, :], T.za[:, :], A.add)
     dma("Y", "xn", "", [(T.yc[:, :], T.xn[:, :])], 2.0)
-    act("pB.u", "pf", T.pf[:, :], T.pB[:, 0:128])
-    dma("S", "pf", "", [(T.yr[:, :], T.pf[:, :])], 2.0)
+    tt("pIA.v rv", "xx", T.xx[:, :], vT, T.rv[:, :], A.max)
+    dma("S", "xx", "", [(T.yr[:, :], T.xx[:, :])], 2.0)
 
     Q = {"V": V, "S": S, "P": P, "G": g, "Y": g.sync}
     cnt = {"V": 0, "S": 0, "P": 0, "G": 0}
@@ -622,10 +697,12 @@ def rank_program(g, core, T, topo):
             evs += readers.get(x, [])
         need(e, evs)
         if o["kind"] == "send":
-            src, dst, sem = o["fn"]
-            g.remote_dma(T[dst][:, :], T[src][:, :], T.sem[sem], T.sem.sent, pid, rid, emask)
+            src, dst, cols = o["fn"]
+            sem = "a" + o["w"][0]
+            g.remote_dma(T[dst][:, cols], T[src][:, cols], T.sem[sem], T.sem.sent, pid, rid, emask)
             sent += neng
-            lastw[dst] = (sem, neng, {})
+            for x in o["w"]:
+                lastw[x] = (sem, neng, {})
             continue
         if o["kind"] == "dma":
             s = "d%d" % len(dmas)

from concourse.mybir import AluOpType, ActivationFunctionType

F32, BF, H, I32, U16 = "float32", "bfloat16", "float16", "int32", "uint16"
W, L, VI = 2048, 128, 4
SCRATCH = {}


def _sb(dtype, cols, names):
    for n in names.split():
        SCRATCH[n] = ("sbuf", [128, cols], dtype)


_sb(BF, 4240, "ZX")
_sb(F32, 4232, "IO")
_sb(I32, 4104, "MX")
_sb(F32, 2184, "TT")
_sb(F32, 2048, "WT Mf")
_sb(I32, 2048, "R0r")
_sb(H, 2048, "Wg Tg MM OH")
_sb(BF, 2048, "Xg Ym ab")
_sb(BF, 2176, "Xm E16")
_sb(BF, 1024, "eq")
_sb(BF, 512, "E1 E3")
_sb(F32, 256, "ta tb")
_sb(H, 128, "z0 z1 z2 z3 zo0 zo1 zo2 zo3 zB")
_sb(I32, 128, "Rin fin pi si qi")
_sb(F32, 128, "krow ones32 I32 Bt mask32 rs1 C0 O32 pf pm diff d1 d2 SCi SCo base LN yy sg sel dz w0 w1 xn xx")
_sb(F32, 144, "rowA D3 rs3 pm3 SV")
_sb(BF, 128, "Ib In BBn KC zero zin nf pen Xn Xc d2b")
_sb(BF, 144, "W1 Wn Wp Wm RR tsp I136 one5 cw")
_sb(H, 128, "k37 m0 idr cn za rv")
_sb(U16, 128, "R0l R0m R0p c0l idL mu su f0 f1 f2 f3 fo0 fo1 fo2 ul")
_sb(U16, 64, "dl")
_sb(I32, 24, "it")
_sb(F32, 128, "cs")
_sb(F32, 64, "q2")
_sb(BF, 64, "Bq Bw")
_sb(I32, 8, "th8")
BANKS = "pD0 pD1 pKA pKB pIA pIB pM pN".split()
for _n in BANKS:
    SCRATCH[_n] = ("psum", [128, 512], F32)

SEMAPHORES = (["sV", "sS", "sP", "sG", "sent"] + ["d%d" % i for i in range(24)]
              + ["a%s%d%d" % (x, v, h) for x in "fz" for v in range(1, VI) for h in range(2)])
LN2 = 0.6931471805599453
OFF = 28672.0
BIG, MID = 2.0 ** 31, 2.0 ** 23
CYC, GATH, SCAT, PECYC, HOP, FAR, FIRST = 0.00104, 1.56, 3.8, 0.00052, 0.10, 3.9, 2.0
ROUNDS, SEED = 10000, 1
OPT = {"x": ["SSSS", "SSSV", "SSSV", "SSSV"], "m": ["SSSS"] * 4, "w": ["", "S-SV", "S-SV", "S-SV"],
       "t": (1, 1, 2), "r0": "S-V-", "xn": "S", "oh": "VVVV", "mm": "S", "parts": ["P-P-"] * 4, "early": 1, "gz": 0, "cut": 4, "cutc": 16, "wt": "VVVV", "end": (0, 8, 12, 14, 16), "zlate": (), "fsplit": (), "front": 1}
ORDER = []


def arrange(ops):
    n = len(ops)
    pred = [set() for _ in ops]
    lastw, readers, lastp, users, closer, queued = {}, {}, {}, {}, {}, set()
    for i, o in enumerate(ops):
        for x in o["r"] + o["w"]:
            if x in lastw:
                pred[i].add(lastw[x])
        for x in o["w"]:
            pred[i].update(readers.get(x, []))
        if o["e"] == "P":
            for b in o["b"]:
                if b in lastp:
                    pred[i].add(lastp[b])
                lastp[b] = i
                if o["open"]:
                    pred[i].update(users.get(b, []))
                    users[b] = []
        else:
            for b in o["b"]:
                users.setdefault(b, []).append(i)
                assert not ops[lastp[b]]["open"], o["w"]
                if closer.get(b) is not None:
                    pred[i].add(closer[b])
        if o["e"] == "P" and o["shut"]:
            closer[o["b"][0]] = i
        if o["e"] in "GY" or o["kind"] == "dma":
            if o["e"] in lastp and lastp[o["e"]] not in pred[i]:
                pred[i].add(lastp[o["e"]])
                queued.add((lastp[o["e"]], i))
            lastp[o["e"]] = i
        for x in o["r"]:
            readers.setdefault(x, []).append(i)
        for x in o["w"]:
            lastw[x] = i
            readers[x] = []
        pred[i].discard(i)
    succ = [[] for _ in ops]
    for i in range(n):
        for j in pred[i]:
            succ[j].append(i)

    def gap(j, i):
        same_queue = ops[j]["e"] == ops[i]["e"] == "P" or (j, i) in queued
        return ops[j]["c"] if same_queue else ops[j]["c"] + ops[j]["lat"]

    c = [o["c"] for o in ops]
    lat = [o["lat"] for o in ops]
    fw = [[(i, gap(j, i)) for i in succ[j]] for j in range(n)]
    bw = [[(j, c[i] + gap(j, i) - c[j]) for j in pred[i]] for i in range(n)]

    def place(key, back):
        after = bw if back else fw
        left = [len(x) for x in (succ if back else pred)]
        at = list(lat) if back else [0.0] * n
        cand = [(key[i], i) for i in range(n) if not left[i]]
        busy = {x: [] for x in list("VSPGY") + BANKS}
        while cand:
            first = min(cand)
            cand.remove(first)
            i = first[1]
            t, ci, e = at[i], c[i], ops[i]["e"]
            q = busy[e]
            lo, hi = (-lat[i], ci) if back else (0.0, ci + lat[i])
            k = len(q)
            while k and q[k - 1][1] > t + 1e-9:
                k -= 1
            moved = True
            while moved:
                while k < len(q) and q[k][0] < t + ci - 1e-9:
                    t = max(t, q[k][1])
                    k += 1
                moved = False
                for x in ops[i]["b"]:
                    for a, b, e2 in reversed(busy[x]):
                        if a < t - 3.0:
                            break
                        if e2 != e and t + lo < b - 1e-9 and t + hi > a + 1e-9:
                            t = b - lo
                            moved = True
            at[i] = t
            q.insert(k, (t, t + ci))
            for x in ops[i]["b"]:
                u = busy[x]
                k = len(u)
                while k and u[k - 1][0] > t + lo:
                    k -= 1
                u.insert(k, (t + lo, t + hi, e))
            for j, d in after[i]:
                if at[j] < t + d:
                    at[j] = t + d
                left[j] -= 1
                if not left[j]:
                    cand.append((key[j], j))
        return at

    prio = [0.0] * n
    for j in range(n - 1, -1, -1):
        prio[j] = max([gap(j, i) + prio[i] for i in succ[j]] + [c[j] + lat[j]])
    visit = [sorted((i for i in range(n) if ops[i]["v"] == v), key=lambda i: ops[i]["w"][:1] != ["pm0"]) for v in range(VI)]
    best, seed = None, SEED
    key = [-x for x in prio]
    for it in range(ROUNDS):
        at = place(key, False)
        span = max(at[i] + c[i] + lat[i] for i in range(n))
        if best is None or span <= best[0]:
            best = (span, at)
        seed = (seed * 1103515245 + 12345) % 2147483648
        mid = seed / 2147483648.0 * best[0]
        late = [-(best[1][i] + c[i]) for i in range(n)]
        if it % 50 == 49:
            a, b = 1 + seed // 64 % 3, 1 + (seed // 64 + 1 + seed // 1024 % 2) % 3
            like = {ops[i]["role"]: late[i] - late[visit[a][0]] for i in visit[a]}
            zero = late[visit[b][0]]
            for i in visit[b]:
                late[i] = like[ops[i]["role"]] + zero if ops[i]["role"] in like else late[i]
            mid = -9.0
        for i in range(n):
            if abs(best[1][i] - mid) < 2.0:
                seed = (seed * 1103515245 + 12345) % 2147483648
                late[i] += (seed / 2147483648.0 - 0.5) * (0.3, 0.8, 2.0, 1.2)[it % 4]
        back = place(late, True)
        key = [-(back[i] + c[i]) for i in range(n)]
    return sorted(range(n), key=lambda i: (best[1][i], i)), best[0]


def rank_program(g, core, T, topo):
    rank = T.rank_of(core)
    if rank is None:
        return
    A, AF = AluOpType, ActivationFunctionType
    nxt = T.cores[(rank + 1) % len(T.cores)]
    rid, pid = topo.addr(nxt, core)
    emask = topo.mask(core, nxt)
    neng = len(topo.engines(core, nxt))
    V, S, P = g.vector, g.scalar, g.tensor
    ops = []
    mark = [0]
    seen, now = {}, [-1]

    def ind(win, off):
        mark[0] = 16 * off.shape[1]
        return win.indirect(off)

    def add(e, r, w, kind, fn, c, lat=HOP):
        r, w = r.split(), w.split()
        b = sorted(set(x.split(".")[0] for x in r + w if "." in x))
        role = (e, w[0][:1] + w[0][-1:] if w and w[0][:2] in ("fo", "zo", "f1", "f2", "f3", "z1", "z2", "z3") else "".join(w[:1]))
        seen[role] = seen.get(role, 0) + 1
        ops.append({"e": e, "r": r, "w": w, "b": b, "kind": kind, "fn": fn, "c": c, "lat": lat, "role": role + (seen[role],), "v": now[0]})

    def op(e, r, w, fn, out, per=1.0, scat=False, more=0.0):
        n, mark[0] = mark[0], 0
        cyc = n * (SCAT if scat else GATH) + 70 if n else max(64, out.shape[1] * per)
        add(e, r, w, "c", fn, cyc * CYC + (0.15 if e == "G" else 0.01) + more)

    def dma(e, r, w, pairs, lat):
        add(e, r, w, "dma", pairs, 0.06 * len(pairs), lat)

    def send(src, dst, h0, h1, lat):
        add("G", names(src, h0, h1), names(dst, h0, h1), "send", (src, dst, slice(64 * h0, 64 * h1)), 0.3, lat)

    def tt(r, w, out, a, b, o, scat=False):
        op("V", r, w, lambda: V.tensor_tensor(out, a, b, o), out, 1.0 if "." in r else 2.0, scat)

    def ts(r, w, out, a, s1, o0, s2=None, o1=None, per=1.0):
        if o1 is None:
            op("V", r, w, lambda: V.tensor_scalar(out, a, s1, None, o0), out, per)
        else:
            op("V", r, w, lambda: V.tensor_scalar(out, a, s1, s2, o0, o1), out, per)

    def cp(r, w, out, a, scat=False):
        op("V", r, w, lambda: V.tensor_copy(out, a), out, 1.0, scat)

    def ms(w, out, c, per=1.0):
        op("V", "", w, lambda: V.memset(out, c), out, per)

    def scan(r, w, out, a, b, o0, o1):
        op("V", r, w, lambda: V.tensor_tensor_scan(out, a, b, 0.0, o0, o1), out)

    def act(r, w, out, a, f=None, more=0.0, **kw):
        op("S", r, w, lambda: S.activation(out, a, AF.Identity if f is None else f, **kw), out, 1.0, False, more)

    def mm(r, w, lst, wide=()):
        def fn():
            ins = None
            for (o, l, rh, st, sp) in lst:
                ins = P.matmul(o, l, rh, st, sp)
            return ins
        cyc = sum(max(min(64, x[1].shape[1]), x[2].shape[1]) * (4 if wide is True or i in wide else 1) for i, x in enumerate(lst))
        add("P", r, w, "c", fn, cyc * PECYC)
        ops[-1]["open"] = not lst[-1][4]
        ops[-1]["shut"] = lst[-1][4] and not lst[0][3]

    def iota(w, out, pat, base, cm, flt=True):
        if flt:
            op("G", "", w, lambda: g.iota(out, pat, base, cm, allow_small_or_imprecise_dtypes=True), out, 2.0)
        else:
            op("G", "", w, lambda: g.iota(out, pat, base, cm), out, 2.0)

    def sel_(r, w, out, a, pat, base, cm):
        op("G", r, w, lambda: g.affine_select(out, a, pat, A.is_equal, 0.0, base, cm), out, 2.0)

    def ch(q, n=512):
        return slice(n * q, n * q + n)

    def names(x, a, b):
        return " ".join("%s%d" % (x, q) for q in range(a, b + (b == 4 and x in ("Tg", "Wg"))))

    ul, o_ = {}, 0
    for n, k in (("dup", 16), ("pick", 8), ("pk2", 8), ("bcq", 8), ("bc3", 8), ("e1", 32), ("e3", 32)):
        ul[n] = T.ul[:, o_:o_ + k]
        o_ += k
    for i, n in enumerate("idl ol idc cmpl sl nl".split()):
        ul[n] = T.dl[:, 8 * i:8 * i + 8]
    cs, o_ = {}, 0
    for n, k in (("k", 1), ("p31", 1), ("p96", 1), ("c3", 1), ("p", 1), ("pk", 1), ("pk0", 1), ("pe", 1), ("p112", 1), ("kp", 1), ("k0", 1),
                 ("t1c", 1), ("t2c", 1), ("t3c", 1), ("v3", 1), ("Ac", 1), ("sc", 1), ("kal", 1), ("t12", 2), ("a1", 1), ("a2", 1), ("t1s", 1), ("pad", 1),
                 ("us", 8), ("cmpv", 8), ("B32", 8), ("t8", 8), ("al", 8), ("c1q", 8), ("nw", 8), ("ix", 8), ("tw", 8), ("fb", 8), ("nx", 8), ("th", 2)):
        cs[n] = T.cs[:, o_:o_ + k]
        o_ += k
    th = cs["th"][0:8, :]
    Bw3, Bb, Bk, Bkn, one_ = T.Bw[:, 0:8], T.Bw[:, 8:16], T.Bw[:, 16:24], T.Bw[:, 24:32], T.Bw[:, 32:40]
    X0 = 2176
    idwin, Xwin, Zout = T.ZX[:, 128:4225], T.ZX[:, X0:4225], T.ZX[:, 0:X0]
    Y = T.Xm[:, 2048:2176]
    Twin, Tout = T.TT[:, 128:2184], T.TT[:, 0:2176]
    IOlo, IOall, IO32 = T.IO[:, 128:2328], T.IO[:, 128:4232], T.IO[:, 160:2208]
    r8, ones = T.rowA[:, 0:8], T.one5[0:1, 0:128]
    ends = slice(15, 128, 16)

    ms("pad", T.ZX[:, X0:X0 + 16], -4096.0)
    for q in range(0 if OPT["gz"] else 4):
        ms("R0r%d" % q, T.R0r[:, ch(q)], 0)
    dma("Y", "", "Rin", [(T.Rin[:, :], T.rep[:, :])], 2.0)
    dma("S", "", "fin0 fin1", [(T.fin[:, :], T.fact[:, :])], 2.0)
    dma("S", "", "zin th8", [(T.zin[:, :], T.z[:, :]), (T.th8[0:8, 0:2], T.thr[:, :])], 2.1)
    dma("Y", "pad", "X pad", [(T.ZX[:, X0 + 1:4225], T.feat[:, :])], 4.0)
    dma("Y", "", "M0", [(T.MX[:, 0:2048], T.memb[:, :])], 8.0)
    dma("Y", "", "Z", [(T.ZX[:, 128:X0], T.feat[:, :])], 10.0)

    iota("it0", T.it[:, 0:1], [[0, 1]], 0, 1, False)
    iota("rowA", T.rowA[:, :], [[1, 144]], 0, 0)
    iota("q2a", T.q2[:, 0:16], [[16, 8], [0, 2]], 0, 0)
    iota("q2b", T.q2[:, 16:48], [[16, 2], [0, 16]], 0, 0)
    iota("krow", T.krow[:, :], [[0, 8], [1, 16]], 0, 0)
    act("rowA", "ones32", T.ones32[:, :], T.rowA[:, 0:128], scale=0.0, bias=1.0)
    act("rowA", "one5", T.one5[:, :], T.rowA[:, :], scale=0.0, bias=1.0)
    sel_("ones32", "Bt", T.Bt[0:8, :], T.ones32[0:8, :], [[1, 8], [0, 16]], 0, -1)
    sel_("one5", "I136", T.I136[:, 0:136], T.one5[:, 0:136], [[16, 8], [1, 17]], -1, -1)
    if OPT["gz"]:
        iota(names("R0r", 0, 4), T.R0r[:, :], [[0, 2048]], 0, 0, False)
    dma("Y", names("R0r", 0, 4), "R0r " + names("R0r", 0, 4), [(T.R0r[0:128:16, :], T.rep[:, :])], 4.0)
    for q, (a, b) in enumerate(((0, 640), (640, 1152), (1152, 1664), (1664, 2328))):
        iota("IO%d" % q, T.IO[:, a:b], [[1, b - a]], a - 128, 0)
    iota("zero", T.zero[:, :], [[0, 128]], 0, 0)
    iota("pen", T.pen[:, :], [[0, 128]], 0, 0)
    iota("tsp", T.tsp[:, :], [[0, 144]], 0, 0)
    iota("Wn", T.Wn[:, :], [[0, 144]], 0, 0)
    iota("SV", T.SV[:, 0:136], [[0, 136]], 0, 16)
    op("G", "SV", "SV", lambda: g.iota(T.SV[:, 0:136:17], [[0, 8]], 2048, 1, allow_small_or_imprecise_dtypes=True), r8, 2.0)
    op("G", "zero", "RR", lambda: g.affine_select(T.RR[:, 0:128], T.zero[:, :], [[-1, 128]], A.not_equal, -MID, 0, 1), T.zero[:, :], 2.0)
    iota("RR2", T.RR[:, 128:144], [[0, 16]], -2 ** 19, 0)

    def upper():
        iota("IO4", T.IO[:, 2328:3280], [[1, 952]], 2200, 0)
        iota("IO5", T.IO[:, 3280:4232], [[1, 952]], 3152, 0)

    if not OPT["gz"]:
        upper()
    lo, hi = names("IO", 0, 4), names("IO", 0, 6)
    dma("Y", lo, "TT", [(T.TT[:, 128:2184], T.IO[:, 129:2185])], 8.0)

    for i, (s1, o0) in enumerate(((15, A.bitwise_and), (31, A.bitwise_and), (96, A.bitwise_and))):
        ts("it0", "it%d" % (i + 1), T.it[:, i + 1:i + 2], T.it[:, 0:1], s1, o0)
    ts("it0", "it4", T.it[:, 4:5], T.it[:, 0:1], 3, A.arith_shift_right, 1, A.bitwise_and)
    cp("it1 it2 it3 it4", "k p31 p96 c3", T.cs[:, 0:4], T.it[:, 1:5])
    ts("q2a k", "dup", ul["dup"], T.q2[:, 0:16], cs["k"], A.add)
    ts("rowA p31", "pick", ul["pick"], r8, 32.0, A.mult, cs["p31"], A.add)

    def turn(r, src, w, dst, lst, plus=0.0):
        cp(r + " dup", "ta", T.ta[:, :], ind(src, ul["dup"]))
        op("V", "ta", "tb", lambda: V.transpose(T.tb[:, :], T.ta[:, :]), T.tb[:, :])
        ts("tb " + lst, w, dst, ind(T.tb[:, :], ul[lst]), plus, A.add)

    act("p96 p31", "p", cs["p"], cs["p96"], bias=cs["p31"])
    act("p96 k", "pe", cs["pe"], cs["p96"], bias=cs["k"])
    act("p k", "p112", cs["p112"], cs["k"], scale=-1.0, bias=cs["p"])
    act("k p31", "pk0", cs["pk0"], cs["k"], scale=31.0, bias=cs["p31"])
    act("c3 pk0", "pk", cs["pk"], cs["c3"], scale=-255.0, bias=cs["pk0"])
    act("k", "kp", cs["kp"], cs["k"], bias=1.0)
    act("k", "kal", cs["kal"], cs["k"], bias=OFF - 128)
    ts("rowA p", "I32", T.I32[:, :], T.rowA[:, 0:128], cs["p"], A.is_equal)
    ts("rowA p112", "B32", cs["B32"], T.rowA[:, 0:128:16], cs["p112"], A.is_equal)
    ts("q2b pe", "e1", ul["e1"], T.q2[:, 16:48], cs["pe"], A.add)
    ts("rowA p96", "e3", ul["e3"], T.rowA[:, 0:32], cs["p96"], A.add)
    ts("rowA pk", "pk2", ul["pk2"], r8, 2.0, A.mult, cs["pk"], A.add)
    cp("rowA", "bcq", ul["bcq"], r8)
    ts("rowA", "bc3", ul["bc3"], r8, 17.0, A.mult, 16.0, A.add)
    ts("krow k", "mask32", T.mask32[:, :], T.krow[:, :], cs["k"], A.is_equal)
    for n, s in (("Ib", 1.0), ("In", -1.0)):
        act("I32", n, T[n][:, :], T.I32[:, :], scale=s)
    act("rowA", "W1", T.W1[:, :], T.rowA[:, :], scale=0.0)
    for n, s in (("Wn", -2048.0), ("W1", 1.0)):
        act("B32", n, T[n][:, 15:143:16], cs["B32"], scale=s)
    act("In e1", "E1", T.E1[:, :], ind(T.In[:, :], ul["e1"]))
    act("In e3", "E3", T.E3[:, :], ind(T.In[:, :], ul["e3"]))
    cp("th8", "th", th, T.th8[0:8, 0:2])
    mm("Bt th", "pM.t", [(T.pM[:, 40:42], T.Bt[0:8, :], th, True, True)], True)
    act("pM.t", "t12", cs["t12"], T.pM[:, 40:42])
    act("t12", "t1c", cs["t1c"], cs["t12"][:, 0:1], scale=2.0 ** 30)
    act("t12", "t1s", cs["t1s"], cs["t12"][:, 0:1], scale=-2.0 ** 20, bias=-63.5 * 2 ** 20)
    act("t12", "Ac", cs["Ac"], cs["t12"][:, 0:1], scale=2.0 ** 20)
    act("krow", "KC", T.KC[0:1, :], T.krow[0:1, :], scale=-65536.0, bias=-32768.0)
    act("krow", "rs1", T.rs1[:, :], T.krow[:, :], scale=2e18, bias=-1e18)
    act("krow", "k37", T.k37[0:1, :], T.krow[0:1, :], scale=1184.0)
    act("t12", "t2c", cs["t2c"], cs["t12"][:, 1:2], bias=0.5)
    act("t12 k", "v3", cs["v3"], cs["t12"][:, 1:2], scale=-4096.0, bias=cs["k"])
    act("I136", "I136", T.I136[:, 0:136:17], T.I136[:, 0:136:17], scale=0.0)
    act("I136 v3", "D3", T.D3[:, 0:136], T.I136[:, 0:136], scale=cs["v3"])
    act("B32", "D3", T.D3[:, 0:136:17], cs["B32"], scale=-MID / 16)
    act("B32", "Bw3", Bw3, cs["B32"], scale=4096.0)
    act("SV", "rs3", T.rs3[:, 0:136], T.SV[:, 0:136], scale=1e17, bias=-2040e17)
    mm("ones32 D3 I32 SV", "pN.c", [(T.pN[:, 0:136], T.ones32[:, :], T.D3[:, 0:136], True, False),
                                    (T.pN[:, 0:136], T.I32[:, :], T.SV[:, 0:136], False, True)], True)
    act("pN.c", "SV", T.SV[:, 0:136], T.pN[:, 0:136])
    mm("Bt", "pN.c", [(T.pN[:, 0:128], T.Bt[0:8, :], T.Bt[0:8, :], True, True)], True)
    act("pN.c", "BBn", T.BBn[:, :], T.pN[:, 0:128], scale=-2048.0)
    act("mask32", "E16a", T.E16[:, 0:128], T.mask32[:, :])
    dma("Y", "E16a one5", "E16", [(T.E16[:, ch(j, 128)], T.E16[:, 0:128] if j < 16 else T.one5[:, 0:128]) for j in range(1, 17)], 6.0)
    act("ones32", "cw", T.cw[0:1, 0:8], T.ones32[0:1, 0:8], scale=-MID)
    act("ones32", "cw", T.cw[0:1, 8:9], T.ones32[0:1, 0:1], scale=0.0)
    act("rowA k", "t8", cs["t8"], r8, scale=16.0, bias=cs["k"])
    act("rowA kal", "al", cs["al"], r8, scale=16.0, bias=cs["kal"])
    act("t8", "c1q", cs["c1q"], cs["t8"], AF.Exp, 1.3, scale=-LN2, bias=63 * LN2)
    act("p c1q", "sc", cs["sc"], cs["p"], AF.Exp, scale=LN2, bias=-64 * LN2)
    for q in range(8):
        act("B32 c1q", "Bq%d" % q, T.Bq[:, ch(q, 8)], cs["B32"], scale=cs["c1q"][:, q:q + 1])

    def diag(out, Wd, src, first, stop):
        return [(out, Wd[:, 15 - r:143 - r], src[:, r:src.shape[1]:16], first and r == 0, stop and r == 15) for r in range(16)]

    def gather(e, r, w, out, src, **kw):
        if e == "V":
            cp(r, w, out, src)
        else:
            act(r, w, out, src, **kw)

    def diff_abs(src, q, E, zA, zn, zlate):
        b = ("pD0", "pD1")[q % 2]
        two = [(zn + " " + E, zA[ch(q, 32), :], T[E][ch(q, 32), :]), ("%s%d Ib" % (src, q), T.Ib[:, :], T[src][:, ch(q)])]
        for i, (r, l, rh) in enumerate(two[::-1] if zlate else two):
            mm(r, b + ".x", [(T[b][:, :], l, rh, i == 0, i == 1)])
        s = 2.0 ** 20 if E == "E1" else 1.0
        act(b + ".x", "ab%d" % q, T.ab[:, ch(q)], T[b][:, :], AF.Abs, scale=s, bias=1024.0 * s)

    PI, PK = ("pIA", "pIB"), ("pKA", "pKB")
    PARTS = {1: ((0, 2),), 2: ((0, 1), (1, 2))}

    def pieces(s):
        cut = [q for q in range(4) if s[q] != "-"] + [4]
        return [(a, b, s[a]) for a, b in zip(cut, cut[1:])]

    def tables():
        turn("Rin", T.Rin[:, :], "R0p", T.R0p[:, :], "pk2", 1.0)
        turn("fin0 fin1", T.fin[:, :], "f00 f01", T.f0[:, :], "pick")
        ts("R0p", "R0l", T.R0l[:, :], T.R0p[:, :], -1.0, A.add, per=0.5)
        ts("R0l", "R0m", T.R0m[:, :], T.R0l[:, :], -1.0, A.mult, 4096.0, A.add, 0.5)
        for a, b, _ in pieces(OPT["oh"]):
            c, l = slice(512 * a, 512 * b), slice(32 * a, 32 * b)
            tt("M0 R0l " + names("IO", a, b), names("OH", a, b), T.OH[:, c], ind(T.MX[:, 0:2048], T.R0l[:, l]), T.IO[:, 128 + 512 * a:128 + 512 * b], A.is_equal)

    def table_W():
        if OPT["gz"]:
            upper()
        for a, b, e in pieces(OPT["wt"]):
            c, l = slice(512 * a, 512 * b), slice(32 * a, 32 * b)
            tt("R0m %s %s" % (names("OH", a, b), hi), names("WT", a, b), T.WT[:, c], ind(IOall, T.R0m[:, l]), T.OH[:, c], A.mult)

    mm("zin Ib", "pM.a", [(T.pM[:, 256:384], T.zin[:, :], T.Ib[:, :], True, True)])
    act("pM.a", "z00 z01", T.z0[:, :], T.pM[:, 256:384], bias=1024.0)
    tables()

    for v in range(VI):
        f, z = "f%d" % v, "z%d" % v
        zB, fa, za_ = T.zB[:, :], names(f, 0, 2), "zB"
        zA, zn = T[z], names(z, 0, 2)
        last = v == VI - 1
        seen.clear()
        now[0] = v
        if v:
            mm(zn + " Ib", "pM.a", [(T.pM[:, 256:384], zA[:, :], T.Ib[:, :], True, True)])
            act("pM.a", "zB", zB, T.pM[:, 256:384])
        else:
            act("zin", "zB", zB, T.zin[:, :], bias=1024.0)
        if v:
            for q0, q1, e in pieces(OPT["w"][v]):
                src, r = ind(T.WT[:, :], T[f][:, 32 * q0:32 * q1]), names("WT", 0, 4) + " " + names(f, q0 // 2, (q1 + 1) // 2)
                if e == "S":
                    act(r, names("Wg", q0, q1), T.Wg[:, 512 * q0:512 * q1], src, scale=1.0 / 2048, bias=-1.0)
                else:
                    ts(r, names("Wg", q0, q1), T.Wg[:, 512 * q0:512 * q1], src, 1.0 / 2048, A.mult, -1.0, A.add)
            for h in range(2):
                for j in range(0, 16, OPT["cutc"]):
                    mm(names("Wg", 2 * h, 2 * h + 2) + " Wn", PI[h] + ".c",
                       diag(T[PI[h]][:, 64:128], T.Wn, T.Wg[:, ch(h, 1024)], True, True)[j:j + OPT["cutc"]])
                ts(PI[h] + ".c", "c0l%d" % h, T.c0l[:, ch(h, 64)], T[PI[h]][:, 64:128], -OFF, A.add)
        q0 = 0
        for n in OPT["t"] if v else ():
            h, cols, lst = q0 // 2, slice(512 * q0, 512 * (q0 + n)), slice(32 * q0, 32 * (q0 + n))
            w = names("Tg", q0, q0 + n)
            tt("TT c0l%d %s" % (h, names("Wg", q0, q0 + n)), w, T.Tg[:, cols], ind(Twin, T.c0l[:, lst]), T.Wg[:, cols], A.min)
            out = T[PI[h]][:, 32 * (q0 % 2):32 * (q0 % 2 + n)]
            reg = " ".join("%s.i%d" % (PI[h], q) for q in range(q0, q0 + n))
            mm(w + " Wn", reg, diag(out, T.Wn, T.Tg[:, cols], True, True))
            ts(reg, names("idL", q0, q0 + n), T.idL[:, lst], out, -OFF, A.add)
            q0 += n
        for q0, q1, e in pieces(OPT["r0"]) if v == 0 else ():
            gather(e, "X pad R0p", names("Ym", q0, q1), T.Ym[:, 512 * q0:512 * q1], ind(Xwin, T.R0p[:, 32 * q0:32 * q1]))
        if v and OPT["early"]:
            tt("yy base sl", "TT", ind(Tout, ul["sl"]), T.yy[:, :], T.base[:, :], A.max, True)
        ts(fa, "O32", T.O32[:, :], T[f][:, :], 32.0, A.mult)
        for h in range(2):
            mm("I32 O32", PI[h] + ".o", [(T[PI[h]][:, 384:448], T.I32[:, :], T.O32[:, ch(h, 64)], True, True)], True)
        for j in range(0, 16, OPT["cut"]):
            mm(za_ + " W1", "pM.u", diag(T.pM[:, 0:8], T.W1, zB, True, True)[j:j + OPT["cut"]])
        act("pM.u", "us", cs["us"], T.pM[:, 0:8], scale=1.0 / 32, bias=-511.0)
        tt("us bcq O32", "pf", T.pf[:, :], ind(cs["us"], ul["bcq"]), T.O32[:, :], A.mult)

        for q0, q1, e in pieces(OPT["x"][v]):
            if v:
                r, src = "Z X pad " + names("idL", q0, q1), ind(idwin, T.idL[:, 32 * q0:32 * q1])
            else:
                r, src = names("Ym", 0, 4) + " " + fa, ind(T.Ym[:, :], T.f0[:, 32 * q0:32 * q1])
            gather(e, r, names("Xg", q0, q1), T.Xg[:, 512 * q0:512 * q1], src)
        for p, (q0, q1, _) in enumerate(pieces(OPT["parts"][v])):
            for q in range(q0, q1):
                diff_abs("Xg", q, "E1", zA, zn, v > 0 and q in OPT["zlate"])
            h, c, c4, e4 = q0 // 2, slice(32 * q0, 32 * q1), slice(2 * q0, 2 * q1), slice(32 * q0 + 15, 32 * q1, 16)
            qn = lambda x: names(x, q0, q1)
            key, kn, i0, n = T[PK[p % 2]][:, c], "%s.k%d" % (PK[p % 2], p), 32 * (q0 % 2), 32 * (q1 - q0)
            mm(qn("ab") + " W1 one5 KC", kn, [(key, ones, T.KC[0:1, c], True, False)] + diag(key, T.W1, T.ab[:, 512 * q0:512 * q1], False, True))
            scan(kn + " rs1", qn("pm"), T.pm[:, c], T.rs1[:, c], key, A.min, A.max)
            tt(kn + " " + qn("pm"), qn("diff"), T.diff[:, c], T.pm[:, c], key, A.subtract)
            tt(PI[h] + ".o " + qn("diff"), qn("d2"), T.d2[:, c], T[PI[h]][:, 384 + i0:384 + i0 + n], T.diff[:, c], A.subtract)
            scan(qn("diff") + " " + qn("d2"), qn("SCo"), T.SCo[:, c], T.diff[:, c], T.d2[:, c], A.min, A.max)
            ts(qn("SCo"), qn("ol"), ul["ol"][:, c4], T.SCo[:, e4], 1.0 / 32, A.mult)
            if v:
                tt(qn(PI[h] + ".i") + " " + qn("diff"), qn("d1"), T.d1[:, c], T[PI[h]][:, i0:i0 + n], T.diff[:, c], A.subtract)
                scan(qn("diff") + " " + qn("d1"), qn("SCi"), T.SCi[:, c], T.diff[:, c], T.d1[:, c], A.min, A.max)
                ts(qn("SCi"), qn("idl"), ul["idl"][:, c4], T.SCi[:, e4], -OFF, A.add)
            else:
                reg, row, out = qn(PI[h] + ".i"), T.Tg[:, 512 * q0:512 * q0 + n], T[PI[h]][:, i0:i0 + n // 16]
                cp("R0r " + qn("ol"), qn("Tg"), row, ind(T.R0r[:, :], ul["ol"][:, c4]))
                mm(qn("Tg") + " W1", reg, diag(out, T.W1, row, True, True))
                cp(reg, qn("idl"), ul["idl"][:, c4], out)
                act(reg, qn("SCi"), T.SCi[:, e4], out, bias=OFF)
            Mwin, mn = (T.MX[:, :], "M0 M1 ") if v else (T.MX[:, 0:2048], "M0 ")
            ts(mn + qn("idl"), qn("mu"), T.mu[:, c], ind(Mwin, ul["idl"][:, c4]), 1.0, A.add)
            ts(qn("mu"), qn("m0"), T.m0[:, c], T.mu[:, c], -1.0, A.add)
            tt("%s %s %s" % (lo, qn("ol"), qn("m0")), qn("pi"), T.pi[:, c], ind(IO32, ul["ol"][:, c4]), T.m0[:, c], A.mult)
            ts(qn("pi"), qn("si"), T.si[:, c], T.pi[:, c], 5, A.arith_shift_right, 2047, A.bitwise_and)
            ts(qn("si"), qn("su"), T.su[:, c], T.si[:, c], 1.0, A.add)
            act(kn + " t1c", qn("nf"), T.nf[:, c], key, AF.Relu, scale=-1024.0, bias=cs["t1c"])
        SCi, pm, m0, idl = (names(x, 0, 4) for x in ("SCi", "pm", "m0", "idl"))

        for h0, h1 in ((0, 1), (1, 2)) if v in OPT["fsplit"] else ((0, 2),):
            c, out = slice(64 * h0, 64 * h1), T.pM[:, 128 + 64 * h0:128 + 64 * h1]
            mm("I32 pf one5 k37 In " + names("nf", 2 * h0, 2 * h1), "pM.f", [(out, T.I32[:, :], T.pf[:, c], True, False),
                                                                     (out, ones, T.k37[0:1, c], False, False),
                                                                     (out, T.In[:, :], T.nf[:, c], False, True)], (0,))
            tt("pM.f O32", "qi", T.qi[:, c], out, T.O32[:, c], A.max)
            ts("qi", names("fin", h0, h1), T.fin[:, c], T.qi[:, c], 5, A.arith_shift_right, 2047, A.bitwise_and)
            if not last:
                cp(names("fin", h0, h1), names("fo%d" % v, h0, h1), T["fo%d" % v][:, c], T.fin[:, c])
                send("fo%d" % v, "f%d" % (v + 1), h0, h1, FAR + (FIRST if v == h0 == 0 else 0.0))
        if last:
            turn("fin0 fin1", T.fin[:, :], "w0", T.w0[:, :], "pick")
            dma("Y", "w0", "", [(T.yo[:, :], T.w0[:, :])], 2.0)

        if v == 0:
            table_W()
        idv = T.SCi[:, ends]
        if v:
            ts(SCi, "idc", ul["idc"], idv, -OFF, A.add, 2048.0, A.min)
            act("TT idc", "pen", T.pen[:, :], ind(Twin, ul["idc"]), AF.Relu, scale=-2 * BIG, bias=BIG)
            act("Z X pad " + idl, "Xc", T.Xc[:, :], ind(idwin, ul["idl"]))
        else:
            act("Z " + idl, "Xc", T.Xc[:, :], ind(T.ZX[:, 128:X0], ul["idl"]))
        act(m0, "base", T.base[:, :], T.m0[:, :], scale=-1.0 / 2048, bias=-1.0 / 2048)
        y_ = T.pN[:, 256:384]
        mm("Xc Ib In " + za_, "pN.b", [(y_, T.In[:, :], zB, True, False), (y_, T.Ib[:, :], T.Xc[:, :], False, True)])
        act("pN.b", "d2b", T.d2b[:, :], y_, AF.Abs, scale=2.0, bias=2048.0)
        mm("d2b Ib In " + za_, "pN.b", [(y_, T.In[:, :], zB, True, False), (y_, T.Ib[:, :], T.d2b[:, :], False, True)])
        act("pN.b", "Y", Y, y_, bias=1024.5)

        act(pm + " Ac", "nw", cs["nw"], T.pm[:, ends], AF.Relu, scale=-1.0, bias=cs["Ac"])
        tt(SCi + " nw", "cmpv", cs["cmpv"], idv, cs["nw"], A.add)
        ts("cmpv", "cmpl", ul["cmpl"], cs["cmpv"], OFF + (4100 if v else 2100), A.min, -OFF, A.add)
        act("cmpl " + (hi if v else lo), "idr", T.idr[:, :], ind(IOall if v else IOlo, ul["cmpl"]), bias=-2048.0)
        a0 = [64 * (q // 4) for q in range(8)]
        for q in range(8):
            ts("idr cmpv", "eq%d" % q, T.eq[:, 128 * q + a0[q]:128 * q + 128], T.idr[:, a0[q]:128], OFF + 2048, A.add,
               cs["cmpv"][:, q:q + 1], A.is_equal, 0.75)
        mm(names("eq", 0, 8) + " " + names("Bq", 0, 8), "pM.v",
           [(T.pM[a0[q]:128, 8:16], T.eq[:, 128 * q + a0[q]:128 * q + 128], T.Bq[:, ch(q, 8)], q == 0, q == 1) for q in (0, 4, 5, 6, 7, 2, 3, 1)])
        act("pM.v sc", "tw", cs["tw"], T.pM[:, 8:16], AF.Abs, scale=cs["sc"], bias=-0.75)
        act("tw", "tsp", T.tsp[:, 15:143:16], cs["tw"], AF.Sign, bias=-0.5)
        act(SCi, "one_", one_, idv, AF.Relu, scale=2.0 ** 20, bias=-2.0 ** 20 * (OFF + 2047.5))
        out = T.pM[:, 16:25]
        mm("one5 cw I32 In one_ " + SCi, "pM.w", [(out, ones, T.cw[0:1, 0:9], True, False), (T.pM[:, 16:24], T.I32[:, :], idv, False, False),
                                                  (T.pM[:, 16:24], T.In[:, :], one_, False, False)], (1,))
        mm("tsp RR RR2", "pM.w", diag(out, T.tsp, T.RR, False, True))
        tt("pM.w al", "ix", cs["ix"], T.pM[:, 16:24], cs["al"], A.max)
        ts("ix", "sl", ul["sl"], cs["ix"], 128 - OFF, A.add)
        if not last:
            act("pM.w Ac", "a1", cs["a1"], T.pM[:, 24:25], bias=cs["Ac"])
            act("a1 t1s", "a2", cs["a2"], cs["a1"], AF.Sign, bias=cs["t1s"])
            act("a1 a2", "Ac", cs["Ac"], cs["a2"], scale=-2.0 ** 26, bias=cs["a1"])


        zo = "zo%d" % v
        for q0, q1, e in pieces(OPT["m"][v]):
            gather(e, "X pad " + names("mu", q0, q1), names("Xm", q0, q1), T.Xm[:, 512 * q0:512 * q1],
                   ind(Xwin, T.mu[:, 32 * q0:32 * q1]))
        key3, kn = T.pKA[:, 128:264], "pKA.3"
        mm("I32 SV", kn, [(key3, T.I32[:, :], T.SV[:, 0:136], True, False)], True)
        for q in range(4):
            h = q // 2
            tt("X pad su%d Xm%d" % (q, q), "Ym%d" % q, T.Ym[:, ch(q)], ind(Xwin, T.su[:, ch(q, 32)]), T.Xm[:, ch(q)], A.min)
            diff_abs("Ym", q, "E3", zA, zn, False)
            if q == 3:
                mm("tsp RR", kn, [(T.pKA[:, 128:264:17], T.RR[:, 0:128], T.tsp[:, 15:143:16], False, False)])
            mm("ab%d Bw3" % q, kn, [(T.pKA[ch(q, 32), 129 + k:129 + k + 7 * 17 + 1:17], T.ab[:, 512 * q + k:512 * q + 512:16], Bw3,
                                     False, False) for k in range(16)])
            if q == 3:
                mm("pen I136", kn, [(key3, T.pen[:, :], T.I136[:, 0:136], False, True)])
            if q % 2:
                eb = T.pKB[:, 256 + 64 * h:320 + 64 * h]
                if h == 0:
                    mm("Ib zero", "pKB.e", [(T.pKB[:, 256:384], T.Ib[:, :], T.zero[:, :], True, False)])
                for j in range(0, 16, OPT["cut"]):
                    mm(names("ab", q - 1, q + 1) + " W1", "pKB.e", diag(eb, T.W1, T.ab[:, ch(h, 1024)], False, False)[j:j + OPT["cut"]])
        mm("Ib pen", "pKB.e", [(T.pKB[:, 256:384], T.Ib[:, :], T.pen[:, :], False, True)])
        act("pKB.e t2c", "sg", T.sg[:, :], T.pKB[:, 256:384], AF.Sign, scale=-1.0, bias=cs["t2c"])
        early = OPT["early"] and not last
        if early:
            tt("sg base sl", "TT", ind(Tout, ul["sl"]), T.sg[:, :], T.base[:, :], A.max, True)
        pm3 = T.pm3[:, 0:136]
        scan(kn + " rs3", "pm3", pm3, T.rs3[:, 0:136], key3, A.max, A.min)
        tt("pm3 bc3 mask32", "LN", T.LN[:, :], ind(pm3, ul["bc3"]), T.mask32[:, :], A.mult)
        out = T.pN[:, 144:152]
        mm("LN B32", "pN.n", [(out, T.LN[:, :], cs["B32"], True, True)], True)
        cp("pN.n", "n1", T.it[:, 8:16], out)
        ts("n1", "n2", T.it[:, 16:24], T.it[:, 8:16], 4095, A.bitwise_and)
        cp("n2", "nl", ul["nl"], T.it[:, 16:24])
        gather(OPT["xn"], names("Xm", 0, 4) + " Y nl", "Xn", T.Xn[:, :], ind(T.Xm[:, :], ul["nl"]))
        out = T.pN[:, 384:512]
        if last:
            mm("Xn Ib zB", "pN.z", [(out, T.Ib[:, :], zB, True, False), (out, T.Ib[:, :], T.Xn[:, :], False, True)])
        else:
            mm("Xn Ib " + zn, "pN.z", [(out, T.Ib[:, :], zA[:, :], True, False), (out, T.Xn[:, :], T.Ib[:, :], False, True)])
        act("pN.z", names(zo, 0, 2), T[zo][:, :], out, scale=0.5, bias=511.75)
        tt("E16 nl base", "cn", T.cn[:, :], ind(T.E16[:, :], ul["nl"]), T.base[:, :], A.mult)
        mm("BBn cn", "pN.c", [(T.pN[:, 0:128], T.BBn[:, :], T.cn[:, :], True, True)])
        tt("pN.c sg", "yy", T.yy[:, :], T.pN[:, 0:128], T.sg[:, :], A.mult)
        if not early:
            tt("yy base sl", "TT", ind(Tout, ul["sl"]), T.yy[:, :], T.base[:, :], A.max, True)
        if not last:
            send(zo, "z%d" % (v + 1), 0, 2, FAR)
            cp("Xn sl", "Z", ind(Zout, ul["sl"]), T.Xn[:, :], True)
        if v == 0:
            iota("M1", T.MX[:, 2048:4104], [[1, 2056]], -1, 0, False)
            iota("Wp", T.Wp[:, :], [[0, 144]], 0, 0)
            iota("Wm", T.Wm[:, :], [[0, 144]], 0, 0)
            act("B32 kp", "Wp", T.Wp[:, 15:143:16], cs["B32"], scale=cs["kp"])
            act("Wp", "Wm", T.Wm[:, 15:143:16], T.Wp[:, 15:143:16], scale=-1.0)
            act("k", "pk0", cs["pk0"], cs["k"], scale=128.0)
            act("rowA pk0", "C0", T.C0[:, :], T.rowA[:, 0:128], bias=cs["pk0"])
        if last:
            act(names(zo, 0, 2), "w1", T.w1[:, :], T[zo][:, :], bias=-1024.0)
            dma("Y", "w1", "", [(T.yz[:, :], T.w1[:, :])], 2.0)

    now[0] = VI
    for q in range(4):
        if OPT["mm"] == "S":
            cp("M0", "Mf%d" % q, T.Mf[:, ch(q)], T.MX[:, ch(q)])
    for q in range(4):
        if OPT["mm"] == "S":
            act(names("Mf", 0, 4) + " R0l", "MM%d" % q, T.MM[:, ch(q)], ind(T.Mf[:, :], T.R0l[:, ch(q, 32)]), bias=1.0)
        else:
            ts("M0 R0l", "MM%d" % q, T.MM[:, ch(q)], ind(T.MX[:, 0:2048], T.R0l[:, ch(q, 32)]), 1.0, A.add)
    vT, sT = T.pIA[:, 128:256], T.pIB[:, 128:256]

    def rows(out, Wd, src, h0, h1, first, stop):
        return [(out, Wd[:, 15 - h:143 - h], src[:, ch(h, 128)], first and h == h0, stop and h == h1 - 1) for h in range(h0, h1)]

    mm(names("MM", 0, 4) + " Wp", "pIB.s", rows(sT, T.Wp, T.MM, 0, 16, True, False))
    mm("In one5", "pIA.v", [(vT, T.In[:, :], T.one5[:, 0:128], True, False)])
    cut = OPT["end"]
    for a, b in zip(cut, cut[1:]):
        part = [h // 4 if h < 14 else 4 for h in range(a, b)]
        c, l = slice(128 * a, 128 * b), slice(8 * a, 8 * b)
        tg, wg = (" ".join("%s%d" % (x, q) for q in sorted(set(part))) for x in ("Tg", "Wg"))
        tt("TT R0l " + names("OH", 0, 4), tg, T.Tg[:, c], ind(Twin, T.R0l[:, l]), T.OH[:, c], A.mult)
        act("TT R0l", wg, T.Wg[:, c], ind(Twin, T.R0l[:, l]), AF.Relu, scale=-2048.0)
        mm(tg + " W1", "pIA.v", rows(vT, T.W1, T.Tg, a, b, False, b == 16))
        mm(wg + " Wm", "pIB.s", rows(sT, T.Wm, T.Wg, a, b, False, b == 16))
    tt("pIA.v C0", "sel", T.sel[:, :], vT, T.C0[:, :], A.is_equal)
    act("pIA.v", "za", T.za[:, :], vT, AF.Relu, scale=-2048.0, bias=-2048.0)
    tt("pIB.s sel", "dz", T.dz[:, :], sT, T.sel[:, :], A.mult)
    act("za", "rv", T.rv[:, :], T.za[:, :], bias=-1.0)
    tt("dz za", "xn", T.xn[:, :], T.dz[:, :], T.za[:, :], A.add)
    dma("Y", "xn", "", [(T.yc[:, :], T.xn[:, :])], 2.0)
    tt("pIA.v rv", "xx", T.xx[:, :], vT, T.rv[:, :], A.max)
    dma("S", "xx", "", [(T.yr[:, :], T.xx[:, :])], 2.0)

    Q = {"V": V, "S": S, "P": P, "G": g, "Y": g.sync}
    cnt = {"V": 0, "S": 0, "P": 0, "G": 0}
    known = {e: {} for e in Q}
    lastw, readers, bank = {}, {}, {}
    dmas, sent = [], 0

    def need(e, evs):
        kn = known[e]
        for s, c, clk in sorted(evs, key=lambda x: -x[1]):
            if kn.get(s, 0) < c:
                Q[e].wait_ge(T.sem[s], c)
                kn[s] = c
                for s2, c2 in clk.items():
                    if kn.get(s2, 0) < c2:
                        kn[s2] = c2

    if not ORDER:
        ORDER.extend(arrange(ops))
    for o in [ops[i] for i in ORDER[0]]:
        e, r, w = o["e"], o["r"], o["w"]
        if o["kind"] == "send":
            w = []
        evs = [ev for b in o["b"] for e2, ev in bank.get(b, {}).items() if e2 != e]
        evs += [lastw[x] for x in r + w if x in lastw and "." not in x]
        for x in w:
            evs += readers.get(x, [])
        need(e, evs)
        if o["kind"] == "send":
            src, dst, cols = o["fn"]
            sem = "a" + o["w"][0]
            g.remote_dma(T[dst][:, cols], T[src][:, cols], T.sem[sem], T.sem.sent, pid, rid, emask)
            sent += neng
            for x in o["w"]:
                lastw[x] = (sem, neng, {})
            continue
        if o["kind"] == "dma":
            s = "d%d" % len(dmas)
            for dst, src in o["fn"]:
                Q[e].dma_start(dst, src).then_inc(T.sem[s], 16)
            ev = (s, 16 * len(o["fn"]), dict(known[e]))
            dmas.append(ev)
        else:
            cnt[e] += 1
            o["fn"]().then_inc(T.sem["s" + e], 1)
            ev = ("s" + e, cnt[e], dict(known[e]))
        for b in o["b"]:
            bank.setdefault(b, {})[e] = ev
        for x in r:
            if "." not in x:
                readers.setdefault(x, []).append(ev)
        for x in w:
            lastw[x] = ev
            readers[x] = []
    need("Y", dmas)
    need("Y", [("s" + e, cnt[e], {}) for e in cnt])
    g.wait_ge(T.sem.sent, sent)
